import numpy as np, ml_dtypes
CORES = [13,21,141,149]
N = 4
BF = ml_dtypes.bfloat16
def gentries(a):
    return np.ascontiguousarray(a.reshape(8, 16, -1).transpose(0, 2, 1)).reshape(8, -1)
def gtable(e):
    e = np.asarray(e); return np.ascontiguousarray(e.reshape(8, -1, 16).transpose(0, 2, 1)).reshape(128, -1).astype(np.int32)
W, R, S, K, M = 2048, 512, 256, 16, 97
V, STEP = W + R, (1, 2, 3, 1)
RO = len(STEP)
def tops(st, s):
    col = np.take_along_axis(st, s[:, :, None], 3); h = np.add.reduce((col > 0).astype(np.int64), axis=2)
    return col, h, np.take_along_axis(col, np.maximum(h - 1, 0)[:, :, None], 2)[:, :, 0]
def aim(b, c):
    return (c - M * b) & (W - 1)
def fill(h, v):
    return np.where(np.arange(16)[:, None] < h, v, 0)
def parts(rng):
    share = np.array([0.0, 0.0, 0.1, 0.1, 0.3, 0.5, 0.8, 0.92])
    q = np.stack([rng.permutation(share) for a in range(N)]).reshape(N, 8, 1, 1); lo = np.stack([rng.permutation(8) for a in range(N)]).reshape(N, 8, 1, 1)
    h = lo + ((17 - lo) * rng.random((N, 8, 1, V))).astype(np.int64); h = np.minimum(np.where(rng.random((N, 8, 1, V)) < q, 16, h), 16)
    v = np.minimum(1 + (255 * rng.random((N, 8, 16, V)) ** rng.choice(np.array([0.5, 1.0, 2.0]), (N, 8, 1, 1))).astype(np.int64), 255)
    first = np.argsort(rng.random((N, 8, 1, V)), axis=-1)[..., :S]; later = W + np.argsort(rng.random((N, 8, RO - 1, R)), axis=-1)[..., :S]
    return fill(h, v), np.concatenate([first, later], axis=2), rng.integers(0, W, (N, 8, RO, K, S))
def pack(st, tr, ca):
    return {"days": np.ascontiguousarray(st.reshape(N, 128, V)).astype(np.float32).astype(BF),
            "trucks": np.stack([gtable(a.reshape(8, -1)) for a in tr]), "cand": np.stack([gtable(a.reshape(8, -1)) for a in ca])}
def setup_inputs(rng):
    return pack(*parts(rng))
def setup_inputs_ties(rng):
    st, tr, ca = parts(rng)
    p = rng.integers(1, 254, (N, 8, 1, 1)); p[0, 0] = 1; p[0, 1] = 253
    v = p + rng.integers(0, 3, st.shape); v[:, 2] = np.broadcast_to(p[:, 2], v[:, 2].shape); st = np.where(st > 0, v, 0)
    ca[:, :, :, K // 2:] = ca[:, :, :, :K // 2]
    e = 1 + np.argsort(rng.random((N, 4, V - 2)), axis=-1)[..., :S]; e[..., 0] = 0; e[..., S - 1] = V - 1; tr[:, 0::2, 0] = e
    e = W + 1 + np.argsort(rng.random((N, 4, RO - 1, R - 2)), axis=-1)[..., :S]; e[..., 0] = V - 1; e[..., S - 1] = W; tr[:, 1::2, 1:] = e
    b = np.roll(tops(st, tr[:, :, 0])[2], STEP[0], axis=0); n = S // 4
    ca[:, :, 0, :, :n] = aim(b[:, :, None, :n], rng.choice(np.array([0, W - 1]), (N, 8, K, n)))
    return pack(st, tr, ca)
def setup_inputs_full(rng):
    st, tr, ca = parts(rng)
    st = fill(np.where(rng.random((N, 8, 1, V)) < 0.8, 16, 15), rng.integers(1, 256, (N, 8, 16, V)))
    for a in range(N):
        for g in range(8):
            x = st[a, g]; s = tr[a, g, 0]
            x[:, s] = np.where(x[:, s] == 0, 7, x[:, s]); x[15, rng.permutation(s)[:S // 2]] = 1
    b = np.roll(tops(st, tr[:, :, 0])[2], STEP[0], axis=0); n = S // 8
    for a in range(N):
        for g in range(8):
            x = st[a, g]; s = tr[a, g, 0]; i = rng.permutation(S); c = ca[a, g, 0]
            rest = rng.permutation(np.setdiff1d(np.arange(W), s)); early, late = rest[:n], rest[n:2 * n]
            x[:, early] = fill(15, 1); x[:, late] = fill(16, 255)
            room = np.setdiff1d(np.nonzero(x[15, :W] == 0)[0], early)
            j = i[:S // 2]; c[:, j] = aim(b[a, g, j], rng.choice(s[s < W], (K, S // 2)))
            j = i[:n]; c[K - 1, j] = aim(b[a, g, j], rng.choice(room, n))
            j = i[S // 2:S // 2 + n]; c[:, j] = aim(b[a, g, j], rng.choice(late, (K, n))); c[K - 1, j] = aim(b[a, g, j], early)
    return pack(st, tr, ca)
def setup_inputs_bare(rng):
    st, tr, ca = parts(rng)
    o = rng.permutation(8); h = rng.integers(0, 4, (N, 8, 1, V)); h[:, o[0]] = 0; h[:, o[1]] = 1; h[:, o[2]] = rng.integers(0, 3, (N, 1, V))
    st = fill(h, rng.integers(1, 256, (N, 8, 16, V)))
    b = np.roll(tops(st, tr[:, :, 0])[2], STEP[0], axis=0)
    for a in range(N):
        for g in o[3:6]:
            s = tr[a, g, 0]; ca[a, g, 0][0] = aim(b[a, g], rng.choice(s[s < W], S))
    return pack(st, tr, ca)
def setup_inputs_crowd(rng):
    st, tr, ca = parts(rng); goals = []; q = int(rng.integers(0, N)); z = (q + STEP[0]) % N
    for a in range(N):
        for g in range(8):
            x = st[a, g]
            if a == z:
                o = int(rng.integers(0, W - S + 1)); o = o - o % S if g < 2 else o
                run = o + rng.permutation(S); x[15, run] = 0
                if g % 2 == 1:
                    tr[a, g, 0] = rng.permutation(run); x[:, run] = fill(rng.integers(1, 16, S), rng.integers(1, 256, S))
            s = tr[a, g, 0]
            if g % 2 == 0 or a == q:
                x[1:, s] = np.where(x[1:, s] > 0, np.maximum(x[1:, s], 2), 0); x[0, s] = 1; x[1, s] = np.maximum(x[1, s], 2)
            if a == z:
                goals.append(run)
            else:
                free = rng.permutation(np.setdiff1d(np.arange(W), s))[:(1, 2, S // 2, 1)[g // 2]]
                if g < 6: x[:, free] = 0
                goals.append(free if g < 6 else s[s < W])
    b = np.roll(tops(st, tr[:, :, 0])[2], STEP[0], axis=0)
    for a in range(N):
        for g in range(8):
            c = ca[a, g, 0]; k = 0 if a == q else int(rng.integers(0, K))
            if a == z: c[:] = aim(b[a, g], goals[8 * a + g])
            elif g < 6: c[k] = aim(b[a, g], rng.choice(goals[8 * a + g], S))
            else: c[:] = aim(b[a, g], rng.choice(goals[8 * a + g], (K, S)))
    ca[:, ::2, 1:] = rng.integers(0, 8, (N, 4, RO - 1, K, S)) + rng.integers(0, W - 8, (N, 4, RO - 1, 1, 1))
    return pack(st, tr, ca)
def setup_inputs_spread(rng):
    st, tr, ca = parts(rng)
    h = np.minimum((17 * rng.random((N, 8, 1, V)) ** rng.choice(np.array([0.2, 0.5, 1.0, 3.0]), (N, 8, 1, 1))).astype(np.int64), 16)
    v = np.minimum(np.maximum((np.exp2(8 * rng.random((N, 8, 1, V))) * rng.random((N, 8, 16, V))).astype(np.int64), 1), 255)
    ca = np.minimum((W * rng.random((N, 8, RO, K, S)) ** rng.choice(np.array([0.5, 1.0, 2.0, 4.0]), (N, 8, RO, 1, 1))).astype(np.int64), W - 1)
    return pack(fill(h, v), tr, ca)
def check_inputs(d):
    bad = []; x = np.asarray(d["days"]).astype(np.float32)
    if not np.all((x >= 0) & (x <= 255) & (x == np.floor(x))): bad.append("days: whole numbers from 0 to 255")
    z = x.reshape(N, 8, 16, V) > 0
    if np.any(z[:, :, 1:] & ~z[:, :, :-1]): bad.append("days: no box above an empty tier")
    s = np.stack([gentries(a) for a in d["trucks"]]).astype(np.int64).reshape(N, 8, RO, S)
    if np.min(s) < 0 or np.max(s) > V - 1 or np.min(s[:, :, 1:]) < W: bad.append("range of trucks")
    o = np.sort(s, axis=-1)
    if np.any(o[..., 1:] == o[..., :-1]): bad.append("trucks: different stacks in a block")
    if np.min(d["cand"]) < 0 or np.max(d["cand"]) > W - 1: bad.append("range of cand")
    return bad
def reference(days, trucks, cand):
    st = np.asarray(days).astype(np.float32).astype(np.int64).reshape(N, 8, 16, V)
    tr = np.stack([gentries(a) for a in trucks]).astype(np.int64).reshape(N, 8, RO, S)
    ca = np.stack([gentries(a) for a in cand]).astype(np.int64).reshape(N, 8, RO, K, S)
    lower = np.tril(np.ones((S, S), bool), -1); s = tr[:, :, 0]
    for t in range(RO):
        col, h, b = tops(st, s)
        asks = np.any((col > 0) & (col < b[:, :, None]), axis=2)
        bb = np.roll(b, STEP[t], axis=0); ask = np.roll(asks, STEP[t], axis=0)
        c = (ca[:, :, t] + M * bb[:, :, None]) & (W - 1)
        cc = np.take_along_axis(st, c.reshape(N, 8, 1, K * S), 3).reshape(N, 8, 16, K, S)
        score = np.add.reduce(((cc > 0) & (cc < bb[:, :, None, None])).astype(np.int64), axis=2) + 16 * (cc[:, :, 15] > 0)
        best = np.argmin(score, axis=2)[:, :, None]
        dst = np.take_along_axis(c, best, 2)[:, :, 0]; low = np.take_along_axis(score, best, 2)[:, :, 0]
        clash = np.any((dst[..., :, None] == dst[..., None, :]) & ask[..., None, :] & lower, axis=3)
        land = ask & (low < 16) & ~clash
        gone = (b > 0) & (~asks | np.roll(land, -STEP[t], axis=0))
        st = st.copy()
        a, g, i = np.nonzero(gone); st[a, g, h[a, g, i] - 1, s[a, g, i]] = 0
        a, g, i = np.nonzero(land); v = dst[a, g, i]
        top = np.add.reduce((st[a, g, :, v] > 0).astype(np.int64), axis=1); st[a, g, top, v] = bb[a, g, i]
        if t + 1 < RO: s = np.where(land, dst, tr[:, :, t + 1])
    return {"y": st.reshape(N, 128, V).astype(np.float32).astype(BF)}

@@ -1,0 +1,528 @@
+from concourse.bass import DstId, RemoteDMATransfer
+from concourse.mybir import AluOpType as Op, AxisListType, ActivationFunctionType as Fn
+
+V, W, SP, DUM, WIN = 2560, 2048, 2560, 2816, 5376
+STEP = (1, 2, 3, 1)
+MS = 12
+NS = 6
+CB0, CB1 = 256, 448
+
+
+def _sb(n, d):
+    return ("sbuf", [128, n], {"b": "bfloat16", "f": "float32", "i": "int32", "u": "uint16"}[d])
+
+
+SCRATCH = {}
+for _d, _l in (("b", dict(S=WIN, pin=2560, yo=2560, zt=2560, I=128, nI=128, tm=128, tn=128, Big=576, BigW=144, BR=512, NP=512, RB=512,
+                          D512=128, D256=128, F=128, SI=896, SO=528, kk=256, c512=256, thr=256, stay=16, pen=64, dS=2048, cmp=4096,
+                          brep=512, EQ=4352, W2=512, val=256, ne=256, em=256, prod=512, crem=256, rl=256, nc=256)),
+               ("f", dict(TRf=64, xi=2064, xs=528, xg=128, xm=256, cf=16, cd=32, wl=16, wn=16, rst=256, wrep=256, msel=256, t1=256,
+                          t2=256, base=64, dif=64, land=64, lm=64, LF=128, o1f=16, b97=16, bq=16, idle=16, K=256, R=256, ef=16,
+                          Df=256, ab=512, sc=256)),
+               ("i", dict(P=1024, TR=64, p4=4, ci=16, X=256, XA=256, ki=32)),
+               ("u", dict(ex=16, ex15=4, LU=64, o1=16, O=256, eu=16, D=256))):
+    for _n, _w in _l.items():
+        SCRATCH[_n] = _sb(_w, _d)
+SCRATCH.update({
+    "dD": ("dram", [8, 128, 320], "bfloat16"), "dA": ("dram", [8, 128, 64], "int32"), "dB": ("dram", [4, 128, 144], "int32"),
+    "aA": ("dram", [8, 128, 64], "int32"), "aB": ("dram", [4, 128, 144], "int32"), "aY": ("dram", [8, 128, 320], "bfloat16"),
+    "hA": ("dram", [128, 64], "int32"), "hB": ("dram", [128, 144], "int32"), "hD": ("dram", [128, 320], "bfloat16"),
+    "hY": ("dram", [128, 320], "bfloat16"),
+})
+for _b in range(8):
+    SCRATCH["B%d" % _b] = ("psum", [128, 512], "float32")
+
+SEMAPHORES = (["cV", "cS", "cT", "cG", "lA", "lX", "lD", "lB", "lS", "lM", "lN", "lT", "s2", "st", "sent", "gA", "gB", "hA", "hB", "hD", "hY"]
+              + ["gD%d" % i for i in range(8)] + ["gY%d" % i for i in range(8)])
+
+
+def _bits(engs):
+    m = 0
+    for e in engs:
+        m |= 1 << e
+    return m
+
+
+def _helpers(T, topo, core):
+    out = {}
+    far = [q for q, c in enumerate(T.cores) if c != core and not topo.may_write(core, c)]
+    for n, q in enumerate(far):
+        own = [c for c in topo.cores_of(core) if T.rank_of(c) is None and topo.may_write(c, T.cores[q])]
+        dies = sorted(set(topo.die(c) for c in own))
+        for h in range(2):
+            same = [c for c in own if topo.die(c) == dies[h % len(dies)]]
+            out[(q, h)] = same[n % len(same)]
+    return out
+
+
+def _helper_program(g, core, T, topo):
+    home = [c for c in topo.cores_of(core) if T.rank_of(c) is not None]
+    if not home:
+        return
+    r = T.rank_of(home[0])
+    jobs = [k for k, c in _helpers(T, topo, home[0]).items() if c == core]
+    if not jobs:
+        return
+    q, h = jobs[0]
+    dst = T.cores[q]
+    rid, pid = topo.addr(dst, core)
+    m = topo.mask(core, dst)
+    n = len(topo.engines(core, dst))
+    steps = [("hA", 2, T.hA[:], T.aA[2 * r + h], "gA"), ("hD", 4, T.hD[:], T.pin[:, 640 * r + 320 * h:640 * r + 320 * h + 320], "gD%d" % (2 * r + h))]
+    if h == 0:
+        steps.append(("hB", 4, T.hB[:], T.aB[r], "gB"))
+    steps.append(("hY", 8, T.hY[:], T.aY[2 * r + h], "gY%d" % (2 * r + h)))
+    for s, cnt, src, out, rs in steps:
+        g.wait_ge(T.sem[s], cnt)
+        g.remote_dma(out, src, T.sem[rs], T.sem.sent, pid, rid, m)
+    g.wait_ge(T.sem.sent, n * len(steps))
+
+
+def rank_program(g, core, T, topo):
+    me = T.rank_of(core)
+    if me is None:
+        _helper_program(g, core, T, topo)
+        return
+    ops = []
+    queue = {"V": g.vector, "S": g.scalar, "T": g.tensor, "G": g, "Y": g.sync}
+
+    def v(name, a=None, b=None, s=1, p=None):
+        t = T[name]
+        if a is None:
+            a, b = 0, t.shape[1]
+        ps = slice(None) if p is None else slice(p[0], p[1])
+        x = t[ps, a:b] if s == 1 else t[ps, a:b:s]
+        p0, p1 = p if p else (0, 128)
+        return (x, [(name, a, b, p0, p1, s == 1)])
+
+    def slot(name, i, a=0, b=128):
+        return (T[name][i] if b - a == 128 else T[name][i, a:b, :], [(name + str(i), a, b, 0, 128, True)])
+
+    def ind(win, off):
+        return (win[0].indirect(off[0]), win[1] + off[1], win[1], off[1])
+
+    def ap(x):
+        return x[0] if isinstance(x, tuple) else x
+
+    def rec(q, fn, outs, ins, sem=None, cnt=0, inc=True):
+        wr, rd = [], []
+        for o in outs:
+            if len(o) == 4:
+                wr += o[2]
+                rd += o[3]
+            else:
+                wr += o[1]
+        for x in ins:
+            if isinstance(x, tuple):
+                rd += x[1]
+        ops.append({"q": q, "fn": fn, "wr": wr, "rd": rd, "sem": sem, "cnt": cnt, "inc": inc})
+
+    def tt(o, a, b, op): rec("V", lambda: g.vector.tensor_tensor(o[0], a[0], b[0], op), [o], [a, b])
+
+    def ts(o, a, s1, op0, s2=None, op1=None):
+        if s2 is None:
+            rec("V", lambda: g.vector.tensor_scalar(o[0], a[0], ap(s1), None, op0), [o], [a, s1])
+        else:
+            rec("V", lambda: g.vector.tensor_scalar(o[0], a[0], ap(s1), ap(s2), op0, op1), [o], [a, s1, s2])
+
+    def cp(o, a): rec("V", lambda: g.vector.tensor_copy(o[0], a[0]), [o], [a])
+    def ms(o, c): rec("V", lambda: g.vector.memset(o[0], c), [o], [])
+    def scan(o, a, b, init, op0, op1): rec("V", lambda: g.vector.tensor_tensor_scan(o[0], a[0], b[0], init, op0, op1), [o], [a, b])
+    def act(o, a, f, bias=0.0, scale=1.0): rec("S", lambda: g.scalar.activation(o[0], a[0], f, ap(bias), ap(scale)), [o], [a, bias, scale])
+    def mm(o, l, r, st, en): rec("T", lambda: g.tensor.matmul(o[0], l[0], r[0], st, en), [o], [l, r])
+
+    def iota(o, pat, base, cm, flag=True):
+        if flag:
+            rec("G", lambda: g.iota(o[0], pat, base, cm, allow_small_or_imprecise_dtypes=True), [o], [])
+        else:
+            rec("G", lambda: g.iota(o[0], pat, base, cm), [o], [])
+
+    def dma(q, o, a, sem): rec(q, lambda: queue[q].dma_start(o[0], a[0]), [o], [a], sem, 16)
+    def arrive(o, sem, cnt): rec(None, None, o, [], sem, cnt)
+    def ext(x): return (x, [])
+
+    def fused(items, ls="sent", outs=()):
+        trs = []
+        for c, engs, src, out, rs in items:
+            rid, pid = topo.addr(c, core)
+            trs.append(RemoteDMATransfer(dst_ids=[DstId(rid=rid, pnc=pid)], dma_engine_mask=_bits(engs), remote_sem=T.sem[rs], src=src[0], dst=out))
+        rec("G", lambda: g.remote_dma_fused(trs, local_sem=T.sem[ls]), list(outs), [it[2] for it in items], ls, sum(len(it[1]) for it in items), False)
+
+    hp = _helpers(T, topo, core)
+    far = sorted(set(q for q, h in hp))
+    near = [q for q in range(len(T.cores)) if q != me and q not in far][0]
+    nc_ = T.cores[near]
+    e_off = topo.engines(core, nc_)
+    e_all = topo.engines(core, hp[(far[0], 0)])
+    e_on = [e for e in e_all if e not in e_off]
+    n_off = len(e_off)
+    hk = [(q, h) for q in far for h in range(2)]
+    others = far + [near]
+    mine = (32 * me, 32 * me + 32)
+    days = lambda q, h: ext(T.days[32 * q:32 * q + 32, 1280 * h:1280 * h + 1280])
+    tile = lambda name, r, h: v(name, 640 * r + 320 * h, 640 * r + 320 * h + 320)
+
+    for q in others:
+        rows = slice(32 * q, 32 * q + 32)
+        dma("Y", slot("dA", 2 * q), ext(T.cand[rows, 0:CB0]), "lA")
+        dma("Y" if q == near else "S", slot("dA", 2 * q + 1, 0, 96), ext(T.cand[rows, CB0:CB1]), "lA")
+        dma("S", slot("dA", 2 * q + 1, 96, 128), ext(T.trucks[rows, :]), "lA")
+    for q, h in hk:
+        dma("Y", slot("dD", 2 * q + h), days(q, h), "lX")
+    for h in range(2):
+        dma("Y", slot("dD", 2 * near + h), days(near, h), "lD")
+    for h in range(2):
+        dma("Y", tile("pin", me, h), days(me, h), "lS")
+    sent_far = (None, [("gate", 0, 1, 0, 128, True)])
+
+    iota(v("p4"), [[32, 4]], 0, 1, False)
+    iota(v("xs"), [[1, 528]], 0, 0)
+    iota(v("xg"), [[16, 8], [0, 16]], 0, 0)
+    iota(v("xm"), [[0, 16], [1, 16]], 0, 0)
+    fused([(hp[k], e_on[2 * n:2 * n + 2], slot("dA", 2 * k[0] + k[1]), T.hA[:], "hA") for n, k in enumerate(hk)]
+          + [(nc_, e_off[4 * h:4 * h + 4], slot("dA", 2 * near + h), T.aA[2 * me + h], "gA") for h in range(2)])
+    fused([(hp[k], e_all[4 * n:4 * n + 4], slot("dD", 2 * k[0] + k[1]), T.hD[:], "hD") for n, k in enumerate(hk)], "s2", [sent_far])
+    fused([(nc_, e_off[4 * h:4 * h + 4], slot("dD", 2 * near + h), tile("pin", me, h)[0], "gD%d" % (2 * me + h)) for h in range(2)])
+    dma("Y", v("TR", 0, 64, p=mine), (T.trucks[mine[0]:mine[1], :], sent_far[1]), "lT")
+    dma("Y", v("P", 0, 1024, p=mine), ext(T.cand[mine[0]:mine[1], :]), "lM")
+    for q in others:
+        dma("Y", slot("dB", q), ext(T.cand[32 * q:32 * q + 32, CB1:1024]), "lB")
+    iota(v("kk"), [[2048, 16], [0, 16]], 0, 0)
+    fused([(hp[(q, 0)], e_on[4 * n:4 * n + 4], slot("dB", q), T.hB[:], "hB") for n, q in enumerate(far)]
+          + [(nc_, e_off, slot("dB", near), T.aB[me], "gB")])
+    iota(v("xi"), [[1, 2064]], 0, 0)
+    iota(v("S", DUM, WIN), [[0, WIN - DUM]], 0, 0)
+
+    arrive([slot("aA", 2 * r + h) for r in others for h in range(2)], "gA", 8 + 4 * n_off)
+    arrive([slot("aB", r) for r in others], "gB", 3 * n_off)
+    for r in others:
+        for h in range(2):
+            arrive([tile("pin", r, h)], "gD%d" % (2 * r + h), 4 if r == near else n_off)
+    for r in others:
+        dma("Y", v("TR", 0, 64, p=(32 * r, 32 * r + 32)), slot("aA", 2 * r + 1, 96, 128), "lT")
+    for r in others:
+        dma("Y", v("P", 0, CB0, p=(32 * r, 32 * r + 32)), slot("aA", 2 * r), "lM")
+    for r in others:
+        dma("Y", v("P", CB0, CB1, p=(32 * r, 32 * r + 32)), slot("aA", 2 * r + 1, 0, 96), "lN")
+    for r in others:
+        dma("Y", v("P", CB1, 1024, p=(32 * r, 32 * r + 32)), slot("aB", r), "lN")
+
+    col = lambda name, j: v(name, j, j + 1)
+    ts(v("ci", 0, 4), v("p4"), 127, Op.bitwise_and)
+    ts(v("ci", 4, 8), v("p4"), 112, Op.bitwise_and)
+    ts(col("ci", 8), col("p4", 0), 15, Op.bitwise_and)
+    ts(col("ci", 9), col("p4", 0), 3, Op.bitwise_and)
+    ts(col("ci", 10), col("p4", 0), 2, Op.logical_shift_right)
+    cp(v("cf", 0, 11), v("ci", 0, 11))
+    pf, rf = col("cf", 0), col("cf", 8)
+    ts(col("cd", 4), col("cf", 10), 96.0, Op.add)
+    ts(v("cd", 12, 16), v("xs", 0, 4), col("cf", 9), Op.is_equal)
+    for j in range(4):
+        ts(v("SI", 224 * j, 224 * j + 224), v("xs", 0, 224), col("cd", 4), Op.is_equal, col("cd", 12 + j), Op.mult)
+    ts(v("cd", 0, 4), v("cf", 4, 8), 15.0, Op.add)
+    ts(col("cd", 5), pf, 4.0, Op.mult, 3.0, Op.add)
+    ts(col("cd", 11), rf, 15.0, Op.is_equal, 256.0, Op.mult)
+    ts(col("cd", 7), pf, -1.0, Op.add)
+    ts(col("cd", 8), pf, 1.0, Op.add)
+    ts(col("cd", 9), rf, 0.0, Op.not_equal, -512.0, Op.mult)
+    ts(col("cd", 10), rf, 15.0, Op.not_equal, 512.0, Op.mult)
+    ts(col("cd", 16), rf, 0.0, Op.is_equal)
+    ts(col("cd", 17), rf, 0.0, Op.not_equal, 256.0, Op.mult)
+    ts(col("cd", 18), rf, 16.0, Op.mult, 15.0, Op.add)
+    ts(col("cd", 6), col("cd", 11), 3840.0, Op.mult, 65536.0, Op.add)
+    act(col("cd", 24), rf, Fn.Sigmoid, 580.0, -40.0)
+    ts(v("I"), v("xs", 0, 128), pf, Op.is_equal)
+    ts(v("nI"), v("xs", 0, 128), pf, Op.is_equal, -1.0, Op.mult)
+    ts(v("tm"), v("xs", 0, 128), pf, Op.is_equal, 512.0, Op.mult)
+    ts(v("tn"), v("xs", 0, 128), col("cd", 7), Op.is_equal, col("cd", 9), Op.mult)
+    ts(v("F"), v("xs", 0, 128), col("cd", 8), Op.is_equal, col("cd", 10), Op.mult)
+    for e in range(4):
+        ts(v("Big", 144 * e, 144 * e + 144), v("xs", 0, 144), col("cd", e), Op.is_equal)
+        ts(v("BR", 128 * e, 128 * e + 128), v("xg"), col("cf", 4 + e), Op.is_equal)
+    tt(v("D512"), v("tm"), v("tn"), Op.add)
+    tt(v("F"), v("F"), v("tm"), Op.subtract)
+    for e in range(1, 4):
+        ts(v("NP", 128 * e, 128 * e + 128), v("xs", 0, 128), col("cf", e), Op.is_equal, -1.0, Op.mult)
+        ts(v("RB", 128 * e, 128 * e + 128), v("xs", 0, 128), col("cf", 4 - e), Op.is_equal, float(DUM), Op.mult)
+    ts(v("D256"), v("D512"), 0.5, Op.mult)
+    ts(v("BigW"), v("xs", 0, 144), col("cd", 0), Op.is_equal, col("cd", 6), Op.mult)
+    ts(v("S", SP, DUM), v("xs", 0, 256), col("cd", 16), Op.mult, col("cd", 17), Op.add)
+    ts(v("ex"), v("xs", 0, 16), 0.0, Op.mult, rf, Op.add)
+    ts(v("ex15"), v("xs", 0, 4), 0.0, Op.mult, col("cd", 18), Op.add)
+    ts(v("lm", 0, 16), v("xs", 0, 16), 16.0, Op.mult, rf, Op.add)
+    ms(v("c512"), 512.0)
+    ms(v("t1"), 1.0 / 1.8)
+    ms(v("t2"), 0.0)
+    ms(v("dif", 48, 64), -256.0)
+    ts(v("base", 0, 16), v("lm", 0, 16), float(DUM), Op.add)
+    ts(v("base", 48, 64), v("lm", 0, 16), 256.0, Op.add)
+    scan(v("wrep"), v("t1"), v("t2"), 1.8e29, Op.mult, Op.add)
+    ts(v("SO"), v("xs"), col("cd", 5), Op.is_equal)
+    ts(v("msel"), v("xm"), rf, Op.is_equal)
+    ts(v("rst"), v("xm"), 0.0, Op.not_equal, -9e29, Op.mult)
+    tt(v("t1"), v("wrep"), v("msel"), Op.mult)
+    rec("V", lambda: g.vector.tensor_reduce(T.cd[:, 19:20], T.t1[:, 0:16], AxisListType.X, Op.add), [col("cd", 19)], [v("t1", 0, 16)])
+    ts(v("thr"), v("t1"), -2.5, Op.mult)
+    ts(col("cd", 20), col("cd", 19), 1e-29, Op.mult)
+    ts(v("wl"), v("wrep", 0, 256, 16), col("cd", 20), Op.mult)
+    ts(v("wn"), v("wl"), -1.0, Op.mult)
+
+    def sel_in(r, h, j, st, en):
+        mm(v("B%d" % (4 * h + j), 0, 320), v("SI", 224 * j + 96 - 32 * r, 224 * j + 224 - 32 * r), tile("pin", r, h), st, en)
+    for r in (me, near):
+        for h in range(2):
+            for j in range(4):
+                sel_in(r, h, j, r == me, False)
+    for h in range(2):
+        for j in range(4):
+            sel_in(far[0], h, j, False, False)
+            sel_in(far[1], h, j, False, True)
+            b = 4 * h + j
+            z = v("zt", 320 * b, 320 * b + 320)
+            act(z, v("B%d" % b, 0, 320), Fn.Relu, 256.0, -256.0)
+            if b == 7:
+                cp(v("LU", 32, 48), v("TR", 0, 16))
+            tt(v("S", 320 * b, 320 * b + 320), v("B%d" % b, 0, 320), z, Op.add)
+
+    I, nI = v("I"), v("nI")
+    Sg, Sw = v("S", 0, DUM), v("S", 0, WIN)
+
+    def listify(out, big, c0, src, a, b, first=True):
+        for r in range(16):
+            mm(out, v(big, c0 + 15 - r, c0 + 143 - r), v(src, a + r, b, 16), first and r == 0, r == 15)
+
+    def tops_a(t):
+        pr = v("prod", 256 * (t % 2), 256 * (t % 2) + 256)
+        mm(v("B0", 0, 256), I, v("val"), True, False)
+        mm(v("B0", 0, 256), v("D512"), v("ne"), False, True)
+        act(pr, v("B0", 0, 256), Fn.Relu, -512.0, 1.0)
+
+    def tops_b(t):
+        e = STEP[t]
+        a = 256 * (t % 2)
+        pr = v("prod", a, a + 256)
+        br = v("BR", 128 * e, 128 * e + 128)
+        mm(v("B2", 0, 256), br, pr, True, True)
+        mm(v("B2", 256, 512), br, pr, True, True)
+        listify(v("B1", 0, 16), "Big", 144 * e, "prod", a, a + 256)
+        mm(v("B0", 256, 512), I, v("val"), True, False)
+        mm(v("B0", 256, 512), v("D256"), v("ne"), False, False)
+        mm(v("B0", 256, 512), nI, pr, False, True)
+        act(v("brep"), v("B2"), Fn.Identity, col("cd", 11), col("cd", 24))
+        act(v("crem") if t == 0 else v("W2", 256, 512), v("B0", 256, 512), Fn.Identity)
+
+    act(v("val"), ind(Sg, v("LU", 32, 48)), Fn.Identity)
+    ts(v("ne"), ind(Sg, v("LU", 32, 48)), 256.0, Op.is_lt)
+    cp(v("TRf"), v("TR"))
+    tops_a(0)
+    tops_b(0)
+    for t in range(4):
+        e, last = STEP[t], t == 3
+        src = v("TRf", 0, 16) if t == 0 else v("LF", 64 * ((t - 1) % 2) + 16, 64 * ((t - 1) % 2) + 32)
+        ts(v("b97"), v("B1", 0, 16), 97.0, Op.mult)
+        for k0, k1 in ((0, NS), (NS, 16)):
+            a, b = 16 * k0, 16 * k1
+            tt(v("X", a, b), ind(v("b97"), v("ex", 0, k1 - k0)), v("P", 256 * t + a, 256 * t + b), Op.add)
+            ts(v("XA", a, b), v("X", a, b), W - 1, Op.bitwise_and)
+            cp(v("O", a, b), v("XA", a, b))
+
+        def gv(k0, k1): tt(v("cmp", 256 * k0, 256 * k1), ind(Sg, v("O", 16 * k0, 16 * k1)), v("brep", 0, 256 * (k1 - k0)), Op.is_lt)
+        def gs(k0, k1): act(v("dS", 256 * k0, 256 * k1), ind(Sg, v("O", 16 * k0, 16 * k1)), Fn.Identity)
+        def df(k0, k1, bk):
+            o = v(bk, 0, 256 * (k1 - k0))
+            mm(o, I, v("brep", 0, 256 * (k1 - k0)), True, False)
+            mm(o, nI, v("dS", 256 * k0, 256 * k1), False, True)
+        def sg(k0, k1, bk): act(v("cmp", 256 * k0, 256 * k1), v(bk, 0, 256 * (k1 - k0)), Fn.Sigmoid, -20.0, 40.0)
+        def score(k0, bk):
+            mm(v(bk, 0, 64), I, v("kk", 16 * k0, 16 * k0 + 64), True, False)
+            if k0 == 4:
+                mm(v(bk, 0, 64), I, v("pen"), False, False)
+            listify(v(bk, 0, 64), "BigW", 0, "cmp", 256 * k0, 256 * k0 + 1024, False)
+        def key(k0, bk): tt(v("K", 16 * k0, 16 * k0 + 64), v(bk, 0, 64), v("X", 16 * k0, 16 * k0 + 64), Op.add)
+
+        gs(0, 2)
+        if t > 0:
+            act(v("crem"), ind(v("W2"), v("LU", 48, 64)), Fn.Identity)
+        df(0, 2, "B3")
+        mm(v("B0", 0, 256), I, v("brep", 0, 256), True, False)
+        mm(v("B0", 0, 256), v("NP", 128 * e, 128 * e + 128), v("crem"), False, True)
+        if t == 0:
+            act(v("rl"), v("B0", 0, 256), Fn.Relu)
+        gs(2, 4)
+        if t > 0:
+            act(v("rl"), v("B0", 0, 256), Fn.Relu)
+        df(2, 4, "B4")
+        listify(v("B2", 0, 16), "Big", 0, "rl", 0, 256)
+        sg(0, 2, "B3"); sg(2, 4, "B4")
+        gv(14, 16); gv(12, 14); gv(10, 12)
+        ts(v("idle"), v("B2", 0, 16), 0.5, Op.is_lt)
+        score(12, "B5")
+        gs(4, 6)
+        score(0, "B6")
+        df(4, 6, "B3")
+        key(12, "B5"); gv(8, 10)
+        ts(v("pen"), ind(v("idle"), v("ex", 0, 4)), float(1 << 21), Op.mult)
+        score(8, "B7"); sg(4, 6, "B3")
+        gv(6, 8); score(4, "B5")
+        mm(v("B3", 0, 256), I, v("thr"), True, False)
+        key(0, "B6")
+        key(8, "B7")
+        tt(v("R", 0, 64), v("K", 0, 64), v("K", 192, 256), Op.min)
+        tt(v("R", 64, 128), v("R", 0, 64), v("K", 128, 192), Op.min)
+        tt(v("R", 128, 160), v("R", 64, 96), v("R", 96, 128), Op.min)
+        key(4, "B5")
+        tt(v("R", 128, 160), v("R", 128, 160), v("pen", 0, 32), Op.add)
+        tt(v("R", 160, 192), v("K", 64, 96), v("K", 96, 128), Op.min)
+        tt(v("R", 192, 224), v("R", 160, 192), v("R", 128, 160), Op.min)
+        tt(v("ki", 0, 16), v("R", 192, 208), v("R", 208, 224), Op.min)
+        ts(v("ki", 16, 32), v("ki", 0, 16), 0x3007FF, Op.bitwise_and)
+        ts(v("eu"), v("ki", 16, 32), float(W), Op.min)
+        if not last:
+            act(v("bq"), v("B1", 0, 16), Fn.Identity, float(SP), 1.0)
+            act(v("base", 16, 32), v("TRf", 16 * t + 16, 16 * t + 32), Fn.Identity)
+            act(v("base", 32, 48), v("TRf", 16 * t + 16, 16 * t + 32), Fn.Identity)
+        ts(v("ef"), v("ki", 16, 32), float(W), Op.min)
+        cp(v("D"), ind(v("xi"), v("eu")))
+        act(v("Df", 0, 256 - 16 * MS), ind(v("xi"), v("eu", MS, 16)), Fn.Identity)
+        eq = lambda m: v("EQ", 272 * m, 256 * m + 256)
+        pos = lambda m: sum(256 - 16 * x for x in range(MS, m))
+        for m in range(MS, 16):
+            act(v("ab", pos(m), pos(m + 1)), v("Df", 16 * (m - MS), 256 - 16 * MS), Fn.Abs, col("ef", m), -1.0)
+        for m in range(MS, 16):
+            act(eq(m), v("ab", pos(m), pos(m + 1)), Fn.Relu, col("wl", m), col("wn", m))
+        for m in range(MS):
+            ts(eq(m), v("D", 16 * m, 256), col("ef", m), Op.is_equal, col("wl", m), Op.mult)
+            mm(v("B3", 16 * m, 256), v("BR", 0, 128), eq(m), False, False)
+        ts(v("EQ", 4096, 4352), v("D"), float(W), Op.is_equal, 1e29, Op.mult)
+        for m in range(MS, 16):
+            mm(v("B3", 16 * m, 256), v("BR", 0, 128), eq(m), False, False)
+        mm(v("B3", 0, 256), v("BR", 0, 128), v("EQ", 4096, 4352), False, True)
+        tt(v("dif", 0, 16), v("ef"), v("base", 0, 16), Op.subtract)
+        if not last:
+            tt(v("dif", 16, 32), v("ef"), v("base", 16, 32), Op.subtract)
+            tt(v("dif", 32, 48), v("bq"), v("base", 32, 48), Op.subtract)
+        n = 16 if last else 64
+        lf = 64 * (t % 2)
+        scan(v("sc"), v("rst"), v("B3", 0, 256), 0.0, Op.max, Op.min)
+        tt(v("stay"), ind(v("sc"), v("ex15", 0, 1)), v("idle"), Op.is_ge)
+        mm(v("B1", 16, 32), v("RB", 128 * e, 128 * e + 128), v("stay"), True, True)
+        mm(v("B6", 0, 256), v("BR", 128 * e, 128 * e + 128), v("prod", 256 * (t % 2), 256 * (t % 2) + 256), True, False)
+        mm(v("B6", 0, 256), I, v("c512"), False, False)
+        ts(v("land", 0, n), ind(v("sc"), v("ex15", 0, n // 16)), 0.0, Op.is_lt)
+        tt(v("o1f"), v("B1", 16, 32), src, Op.add)
+        tt(v("lm", 0, n), v("land", 0, n), v("dif", 0, n), Op.mult)
+        cp(v("o1"), v("o1f"))
+        tt(v("LF", lf, lf + n), v("lm", 0, n), v("base", 0, n), Op.add)
+        cp(ind(Sw, v("o1")), v("crem"))
+        cp(v("LU", 0, n), v("LF", lf, lf + n))
+        cp(v("W2", 0, 256), ind(Sg, v("eu")))
+        if not last:
+            act(v("val"), ind(Sg, v("LU", 32, 48)), Fn.Identity)
+            act(v("ne"), v("val"), Fn.Sign, 256.0, -1.0)
+        ts(v("em"), v("W2", 0, 256), 256.0, Op.is_ge)
+        mm(v("B6", 0, 256), v("F"), v("em"), False, True)
+        if not last:
+            tops_a(t + 1)
+        tt(v("nc"), v("B6", 0, 256), v("W2", 0, 256), Op.min)
+        cp(ind(Sw, v("LU", 0, 16)), v("nc"))
+        if not last:
+            tops_b(t + 1)
+
+    n = 0
+    home = lambda r, h: ext(T.y[32 * r:32 * r + 32, 1280 * h:1280 * h + 1280])
+    for r in far + [near, me]:
+        for h in range(2):
+            bk = v("B%d" % (n % 8), 0, 320)
+            for j in range(4):
+                c = 1280 * h + 320 * j
+                mm(bk, v("SO", 128 * r + 3 - j, 128 * r + 131 - j), v("S", c, c + 320), j == 0, j == 3)
+            z = v("zt", 320 * n, 320 * n + 320)
+            act(z, bk, Fn.Relu, 65536.0, -256.0)
+            tt(tile("yo", r, h), bk, z, Op.min)
+            n += 1
+        if r in far:
+            fused([(hp[(r, h)], e_all[8 * h:8 * h + 8], tile("yo", r, h), T.hY[:], "hY") for h in range(2)])
+        elif r == near:
+            fused([(nc_, e_off[4 * h:4 * h + 4], tile("yo", r, h), T.aY[2 * me + h], "gY%d" % (2 * me + h)) for h in range(2)])
+        else:
+            for h in range(2):
+                dma("S", home(me, h), tile("yo", me, h), "st")
+    for r in far + [near]:
+        for h in range(2):
+            arrive([slot("aY", 2 * r + h)], "gY%d" % (2 * r + h), 4 if r == near else n_off)
+            dma("Y" if h == 0 else "S", home(r, h), slot("aY", 2 * r + h), "st")
+    _emit(g, T, ops, queue)
+
+
+def _emit(g, T, ops, queue):
+    total, log = {}, {}
+    for o in ops:
+        if o["sem"]:
+            total[o["sem"]] = total.get(o["sem"], 0) + o["cnt"]
+    known = {q: {} for q in queue}
+    for i, o in enumerate(ops):
+        q = o["q"]
+        need = []
+        for regs, wr in ((o["rd"], False), (o["wr"], True)):
+            for nm, a, b, p0, p1, full in regs:
+                ps = nm[0] == "B" and nm[1:].isdigit()
+                for j, a2, b2, r0, r1, w2 in log.get(nm, []):
+                    if j == i:
+                        continue
+                    if ps:
+                        hit = ops[j]["q"] != q
+                    else:
+                        hit = (wr or w2) and a < b2 and a2 < b and p0 < r1 and r0 < p1
+                    if hit:
+                        need.append(j)
+        for regs, wr in ((o["rd"], False), (o["wr"], True)):
+            for nm, a, b, p0, p1, full in regs:
+                ps = nm[0] == "B" and nm[1:].isdigit()
+                old = log.get(nm, [])
+                if ps:
+                    old = [x for x in old if ops[x[0]]["q"] == q and q != "T"]
+                elif wr and full:
+                    old = [x for x in old if not (a <= x[1] and x[2] <= b and p0 <= x[3] and x[4] <= p1)]
+                log[nm] = old + [(i, a, b, p0, p1, wr)]
+        o["waits"] = []
+        if q is not None:
+            kn = known[q]
+            top = {}
+            for j in need:
+                d = ops[j]
+                if d["sem"]:
+                    top[d["sem"]] = j
+                else:
+                    if d["q"] != "T":
+                        d["mark"] = True
+                    top["c" + d["q"]] = max(top.get("c" + d["q"], -1), j)
+            for s, j in sorted(top.items(), key=lambda x: -x[1]):
+                lvl = 10 ** 9 if ops[j]["sem"] else j
+                if kn.get(s, -1) >= lvl:
+                    continue
+                ops[j]["mark"] = True
+                o["waits"].append((s, j))
+                kn[s] = lvl
+                if not ops[j]["sem"]:
+                    for s2, l2 in ops[j]["clock"].items():
+                        kn[s2] = max(kn.get(s2, -1), l2)
+            o["clock"] = dict(kn)
+    cnt = {}
+    for o in ops:
+        if not o["sem"] and o.get("mark"):
+            s = "c" + o["q"]
+            cnt[s] = cnt.get(s, 0) + 1
+            o["n"] = cnt[s]
+    for o in ops:
+        if o["q"] is None:
+            continue
+        for s, j in o["waits"]:
+            queue[o["q"]].wait_ge(T.sem[s], total[s] if ops[j]["sem"] else ops[j]["n"])
+        ins = o["fn"]()
+        if o["sem"]:
+            if o["inc"]:
+                ins.then_inc(T.sem[o["sem"]], 16)
+        elif o.get("mark"):
+            ins.then_inc(T.sem["c" + o["q"]], 1)
+    for s, n in list(cnt.items()) + list(total.items()):
+        g.wait_ge(T.sem[s], n)

@@ -5,7 +5,6 @@ V, W, SP, DUM, WIN = 2560, 2048, 2560, 2816, 5376
 STEP = (1, 2, 3, 1)
 MS = 12
 NS = 6
-CB0, CB1 = 256, 448
 
 
 def _sb(n, d):
@@ -15,25 +14,26 @@ def _sb(n, d):
 SCRATCH = {}
 for _d, _l in (("b", dict(S=WIN, pin=2560, yo=2560, zt=2560, I=128, nI=128, tm=128, tn=128, Big=576, BigW=144, BR=512, NP=512, RB=512,
                           D512=128, D256=128, F=128, SI=896, SO=528, kk=256, c512=256, thr=256, stay=16, pen=64, dS=2048, cmp=4096,
-                          brep=512, EQ=4352, W2=512, val=256, ne=256, em=256, prod=512, crem=256, rl=256, nc=256)),
-               ("f", dict(TRf=64, xi=2064, xs=528, xg=128, xm=256, cf=16, cd=32, wl=16, wn=16, rst=256, wrep=256, msel=256, t1=256,
-                          t2=256, base=64, dif=64, land=64, lm=64, LF=128, o1f=16, b97=16, bq=16, idle=16, K=256, R=256, ef=16,
-                          Df=256, ab=512, sc=256)),
+                          brep=512, EQ=4096, W2=512, val=256, ne=256, em=256, prod=512, crem=256, rl=256, nc=256)),
+               ("f", dict(If=128, vt=64, vs=16, Xf=64, TRf=64, xi=2064, xs=528, xg=128, xm=256, cf=16, cd=32, wl=16, wn=16, rst=256,
+                          wrep=256, msel=256, t1=256, t2=256, base=64, dif=64, land=64, lm=64, LF=128, b97=16, bq=16, idle=16, K=256,
+                          R=256, ef=16, Df=256, ab=512, sc=256)),
                ("i", dict(P=1024, TR=64, p4=4, ci=16, X=256, XA=256, ki=32)),
                ("u", dict(ex=16, ex15=4, LU=64, o1=16, O=256, eu=16, D=256))):
     for _n, _w in _l.items():
         SCRATCH[_n] = _sb(_w, _d)
+for _n, _w in (("T", 8), ("A", 32), ("B", 96)):
+    SCRATCH.update({"d" + _n: ("dram", [8, 128, _w], "int32"), "a" + _n: ("dram", [8, 128, _w], "int32"), "h" + _n: ("dram", [128, _w], "int32")})
 SCRATCH.update({
-    "dD": ("dram", [8, 128, 320], "bfloat16"), "dA": ("dram", [8, 128, 64], "int32"), "dB": ("dram", [4, 128, 144], "int32"),
-    "aA": ("dram", [8, 128, 64], "int32"), "aB": ("dram", [4, 128, 144], "int32"), "aY": ("dram", [8, 128, 320], "bfloat16"),
-    "hA": ("dram", [128, 64], "int32"), "hB": ("dram", [128, 144], "int32"), "hD": ("dram", [128, 320], "bfloat16"),
-    "hY": ("dram", [128, 320], "bfloat16"),
+    "dD": ("dram", [8, 128, 320], "bfloat16"), "aY": ("dram", [8, 128, 320], "bfloat16"),
+    "dN": ("dram", [128, 640], "bfloat16"), "aN": ("dram", [128, 640], "bfloat16"),
+    "hD": ("dram", [128, 320], "bfloat16"), "hY": ("dram", [128, 320], "bfloat16"),
 })
 for _b in range(8):
     SCRATCH["B%d" % _b] = ("psum", [128, 512], "float32")
 
-SEMAPHORES = (["cV", "cS", "cT", "cG", "lA", "lX", "lD", "lB", "lS", "lM", "lN", "lT", "s2", "st", "sent", "gA", "gB", "hA", "hB", "hD", "hY"]
-              + ["gD%d" % i for i in range(8)] + ["gY%d" % i for i in range(8)])
+SEMAPHORES = (["cV", "cS", "cT", "cG", "lA", "lC", "lX", "lD", "lB", "lS", "lM", "lN", "lT", "s2", "st", "sent", "gA", "gB", "gT", "hT",
+               "hA", "hB", "hD", "hY"] + ["gD%d" % i for i in range(8)] + ["gY%d" % i for i in range(8)])
 
 
 def _bits(engs):
@@ -68,10 +68,9 @@ def _helper_program(g, core, T, topo):
     rid, pid = topo.addr(dst, core)
     m = topo.mask(core, dst)
     n = len(topo.engines(core, dst))
-    steps = [("hA", 2, T.hA[:], T.aA[2 * r + h], "gA"), ("hD", 4, T.hD[:], T.pin[:, 640 * r + 320 * h:640 * r + 320 * h + 320], "gD%d" % (2 * r + h))]
-    if h == 0:
-        steps.append(("hB", 4, T.hB[:], T.aB[r], "gB"))
-    steps.append(("hY", 8, T.hY[:], T.aY[2 * r + h], "gY%d" % (2 * r + h)))
+    k = 2 * r + h
+    steps = [("hT", 2, T.hT[:], T.aT[k], "gT"), ("hD", 4, T.hD[:], T.pin[:, 320 * k:320 * k + 320], "gD%d" % k),
+             ("hA", 2, T.hA[:], T.aA[k], "gA"), ("hB", 2, T.hB[:], T.aB[k], "gB"), ("hY", 8, T.hY[:], T.aY[k], "gY%d" % k)]
     for s, cnt, src, out, rs in steps:
         g.wait_ge(T.sem[s], cnt)
         g.remote_dma(out, src, T.sem[rs], T.sem.sent, pid, rid, m)
@@ -95,8 +94,8 @@ def rank_program(g, core, T, topo):
         p0, p1 = p if p else (0, 128)
         return (x, [(name, a, b, p0, p1, s == 1)])
 
-    def slot(name, i, a=0, b=128):
-        return (T[name][i] if b - a == 128 else T[name][i, a:b, :], [(name + str(i), a, b, 0, 128, True)])
+    def slot(name, i, n=1):
+        return (T[name][i] if n == 1 else T[name][i:i + n], [(name + "_", i, i + n, 0, 128, True)])
 
     def ind(win, off):
         return (win[0].indirect(off[0]), win[1] + off[1], win[1], off[1])
@@ -149,7 +148,7 @@ def rank_program(g, core, T, topo):
         rec("G", lambda: g.remote_dma_fused(trs, local_sem=T.sem[ls]), list(outs), [it[2] for it in items], ls, sum(len(it[1]) for it in items), False)
 
     hp = _helpers(T, topo, core)
-    far = sorted(set(q for q, h in hp))
+    far = sorted(set(q for q, h in hp), key=lambda q: (q - me) % len(T.cores))
     near = [q for q in range(len(T.cores)) if q != me and q not in far][0]
     nc_ = T.cores[near]
     e_off = topo.engines(core, nc_)
@@ -162,15 +161,15 @@ def rank_program(g, core, T, topo):
     days = lambda q, h: ext(T.days[32 * q:32 * q + 32, 1280 * h:1280 * h + 1280])
     tile = lambda name, r, h: v(name, 640 * r + 320 * h, 640 * r + 320 * h + 320)
 
-    for q in others:
-        rows = slice(32 * q, 32 * q + 32)
-        dma("Y", slot("dA", 2 * q), ext(T.cand[rows, 0:CB0]), "lA")
-        dma("Y" if q == near else "S", slot("dA", 2 * q + 1, 0, 96), ext(T.cand[rows, CB0:CB1]), "lA")
-        dma("S", slot("dA", 2 * q + 1, 96, 128), ext(T.trucks[rows, :]), "lA")
+    def yards(x):
+        fused([(hp[k], e_on[2 * n:2 * n + 2], slot("d" + x, 2 * k[0] + k[1]), T["h" + x][:], "h" + x) for n, k in enumerate(hk)]
+              + [(nc_, e_off[4 * h:4 * h + 4], slot("d" + x, 2 * near + h), T["a" + x][2 * me + h], "g" + x) for h in range(2)])
+    dma("S", slot("dT", 0, 8), ext(T.trucks[:, :]), "lC")
     for q, h in hk:
         dma("Y", slot("dD", 2 * q + h), days(q, h), "lX")
     for h in range(2):
-        dma("Y", slot("dD", 2 * near + h), days(near, h), "lD")
+        dma("Y", v("dN", 320 * h, 320 * h + 320), days(near, h), "lD")
+    dma("Y", slot("dA", 0, 8), ext(T.cand[:, 0:256]), "lA")
     for h in range(2):
         dma("Y", tile("pin", me, h), days(me, h), "lS")
     sent_far = (None, [("gate", 0, 1, 0, 128, True)])
@@ -178,34 +177,32 @@ def rank_program(g, core, T, topo):
     iota(v("p4"), [[32, 4]], 0, 1, False)
     iota(v("xs"), [[1, 528]], 0, 0)
     iota(v("xg"), [[16, 8], [0, 16]], 0, 0)
-    iota(v("xm"), [[0, 16], [1, 16]], 0, 0)
-    fused([(hp[k], e_on[2 * n:2 * n + 2], slot("dA", 2 * k[0] + k[1]), T.hA[:], "hA") for n, k in enumerate(hk)]
-          + [(nc_, e_off[4 * h:4 * h + 4], slot("dA", 2 * near + h), T.aA[2 * me + h], "gA") for h in range(2)])
+    yards("T")
     fused([(hp[k], e_all[4 * n:4 * n + 4], slot("dD", 2 * k[0] + k[1]), T.hD[:], "hD") for n, k in enumerate(hk)], "s2", [sent_far])
-    fused([(nc_, e_off[4 * h:4 * h + 4], slot("dD", 2 * near + h), tile("pin", me, h)[0], "gD%d" % (2 * me + h)) for h in range(2)])
+    fused([(nc_, e_off, (T.dN[:], v("dN")[1]), T.pin[:, 640 * me:640 * me + 640], "gD%d" % (2 * me))])
+    yards("A")
     dma("Y", v("TR", 0, 64, p=mine), (T.trucks[mine[0]:mine[1], :], sent_far[1]), "lT")
     dma("Y", v("P", 0, 1024, p=mine), ext(T.cand[mine[0]:mine[1], :]), "lM")
     for q in others:
-        dma("Y", slot("dB", q), ext(T.cand[32 * q:32 * q + 32, CB1:1024]), "lB")
+        dma("Y", slot("dB", 2 * q, 2), ext(T.cand[32 * q:32 * q + 32, 256:1024]), "lB")
+    iota(v("xm"), [[0, 16], [1, 16]], 0, 0)
     iota(v("kk"), [[2048, 16], [0, 16]], 0, 0)
-    fused([(hp[(q, 0)], e_on[4 * n:4 * n + 4], slot("dB", q), T.hB[:], "hB") for n, q in enumerate(far)]
-          + [(nc_, e_off, slot("dB", near), T.aB[me], "gB")])
     iota(v("xi"), [[1, 2064]], 0, 0)
+    yards("B")
     iota(v("S", DUM, WIN), [[0, WIN - DUM]], 0, 0)
 
-    arrive([slot("aA", 2 * r + h) for r in others for h in range(2)], "gA", 8 + 4 * n_off)
-    arrive([slot("aB", r) for r in others], "gB", 3 * n_off)
-    for r in others:
+    for x in "TAB":
+        arrive([slot("a" + x, 2 * r, 2) for r in others], "g" + x, 8 + 4 * n_off)
+    arrive([tile("pin", near, 0), tile("pin", near, 1)], "gD%d" % (2 * near), n_off)
+    for r in far:
         for h in range(2):
-            arrive([tile("pin", r, h)], "gD%d" % (2 * r + h), 4 if r == near else n_off)
+            arrive([tile("pin", r, h)], "gD%d" % (2 * r + h), n_off)
     for r in others:
-        dma("Y", v("TR", 0, 64, p=(32 * r, 32 * r + 32)), slot("aA", 2 * r + 1, 96, 128), "lT")
+        dma("Y", v("TR", 0, 64, p=(32 * r, 32 * r + 32)), slot("aT", 2 * r, 2), "lT")
     for r in others:
-        dma("Y", v("P", 0, CB0, p=(32 * r, 32 * r + 32)), slot("aA", 2 * r), "lM")
+        dma("Y", v("P", 0, 256, p=(32 * r, 32 * r + 32)), slot("aA", 2 * r, 2), "lM")
     for r in others:
-        dma("Y", v("P", CB0, CB1, p=(32 * r, 32 * r + 32)), slot("aA", 2 * r + 1, 0, 96), "lN")
-    for r in others:
-        dma("Y", v("P", CB1, 1024, p=(32 * r, 32 * r + 32)), slot("aB", r), "lN")
+        dma("Y", v("P", 256, 1024, p=(32 * r, 32 * r + 32)), slot("aB", 2 * r, 2), "lN")
 
     col = lambda name, j: v(name, j, j + 1)
     ts(v("ci", 0, 4), v("p4"), 127, Op.bitwise_and)
@@ -232,6 +229,7 @@ def rank_program(g, core, T, topo):
     ts(col("cd", 6), col("cd", 11), 3840.0, Op.mult, 65536.0, Op.add)
     act(col("cd", 24), rf, Fn.Sigmoid, 580.0, -40.0)
     ts(v("I"), v("xs", 0, 128), pf, Op.is_equal)
+    ts(v("If"), v("xs", 0, 128), pf, Op.is_equal)
     ts(v("nI"), v("xs", 0, 128), pf, Op.is_equal, -1.0, Op.mult)
     ts(v("tm"), v("xs", 0, 128), pf, Op.is_equal, 512.0, Op.mult)
     ts(v("tn"), v("xs", 0, 128), col("cd", 7), Op.is_equal, col("cd", 9), Op.mult)
@@ -287,29 +285,32 @@ def rank_program(g, core, T, topo):
     I, nI = v("I"), v("nI")
     Sg, Sw = v("S", 0, DUM), v("S", 0, WIN)
 
-    def listify(out, big, c0, src, a, b, first=True):
+    def listify(out, big, c0, src, a, b, first=True, end=True):
         for r in range(16):
-            mm(out, v(big, c0 + 15 - r, c0 + 143 - r), v(src, a + r, b, 16), first and r == 0, r == 15)
+            mm(out, v(big, c0 + 15 - r, c0 + 143 - r), v(src, a + r, b, 16), first and r == 0, end and r == 15)
 
     def tops_a(t):
         pr = v("prod", 256 * (t % 2), 256 * (t % 2) + 256)
         mm(v("B0", 0, 256), I, v("val"), True, False)
         mm(v("B0", 0, 256), v("D512"), v("ne"), False, True)
         act(pr, v("B0", 0, 256), Fn.Relu, -512.0, 1.0)
+        mm(v("B7", 0, 256), I, v("val"), True, False)
+        mm(v("B7", 0, 256), v("D256"), v("ne"), False, False)
+        mm(v("B7", 0, 256), nI, pr, False, True)
+        act(v("crem") if t == 0 else v("W2", 256, 512), v("B7", 0, 256), Fn.Identity)
 
     def tops_b(t):
         e = STEP[t]
         a = 256 * (t % 2)
         pr = v("prod", a, a + 256)
         br = v("BR", 128 * e, 128 * e + 128)
+        listify(v("B1", 0, 16), "Big", 144 * e, "prod", a, a + 256)
         mm(v("B2", 0, 256), br, pr, True, True)
         mm(v("B2", 256, 512), br, pr, True, True)
-        listify(v("B1", 0, 16), "Big", 144 * e, "prod", a, a + 256)
-        mm(v("B0", 256, 512), I, v("val"), True, False)
-        mm(v("B0", 256, 512), v("D256"), v("ne"), False, False)
-        mm(v("B0", 256, 512), nI, pr, False, True)
+        act(v("b97"), v("B1", 0, 16), Fn.Identity, 0.0, 97.0)
+        if t > 0:
+            act(v("crem"), ind(v("W2"), v("LU", 48, 64)), Fn.Identity)
         act(v("brep"), v("B2"), Fn.Identity, col("cd", 11), col("cd", 24))
-        act(v("crem") if t == 0 else v("W2", 256, 512), v("B0", 256, 512), Fn.Identity)
 
     act(v("val"), ind(Sg, v("LU", 32, 48)), Fn.Identity)
     ts(v("ne"), ind(Sg, v("LU", 32, 48)), 256.0, Op.is_lt)
@@ -318,12 +319,14 @@ def rank_program(g, core, T, topo):
     tops_b(0)
     for t in range(4):
         e, last = STEP[t], t == 3
+        n = 16 if last else 64
         src = v("TRf", 0, 16) if t == 0 else v("LF", 64 * ((t - 1) % 2) + 16, 64 * ((t - 1) % 2) + 32)
-        ts(v("b97"), v("B1", 0, 16), 97.0, Op.mult)
-        for k0, k1 in ((0, NS), (NS, 16)):
-            a, b = 16 * k0, 16 * k1
-            tt(v("X", a, b), ind(v("b97"), v("ex", 0, k1 - k0)), v("P", 256 * t + a, 256 * t + b), Op.add)
+        parts = ((0, 16 * NS), (16 * NS, 256))
+        for a, b in parts:
+            tt(v("X", a, b), ind(v("b97"), v("ex", 0, (b - a) // 16)), v("P", 256 * t + a, 256 * t + b), Op.add)
+        for a, b in parts:
             ts(v("XA", a, b), v("X", a, b), W - 1, Op.bitwise_and)
+        for a, b in ((0, 96), (192, 256), (96, 192)):
             cp(v("O", a, b), v("XA", a, b))
 
         def gv(k0, k1): tt(v("cmp", 256 * k0, 256 * k1), ind(Sg, v("O", 16 * k0, 16 * k1)), v("brep", 0, 256 * (k1 - k0)), Op.is_lt)
@@ -335,45 +338,45 @@ def rank_program(g, core, T, topo):
         def sg(k0, k1, bk): act(v("cmp", 256 * k0, 256 * k1), v(bk, 0, 256 * (k1 - k0)), Fn.Sigmoid, -20.0, 40.0)
         def score(k0, bk):
             mm(v(bk, 0, 64), I, v("kk", 16 * k0, 16 * k0 + 64), True, False)
-            if k0 == 4:
+            if k0 != 12:
                 mm(v(bk, 0, 64), I, v("pen"), False, False)
-            listify(v(bk, 0, 64), "BigW", 0, "cmp", 256 * k0, 256 * k0 + 1024, False)
+            if k0 == 4:
+                mm(v(bk, 0, 64), v("If"), v("Xf"), False, False)
+            listify(v(bk, 0, 64), "BigW", 0, "cmp", 256 * k0, 256 * k0 + 1024, False, k0 != 12)
+            if k0 == 12:
+                mm(v(bk, 0, 64), I, v("pen"), False, True)
         def key(k0, bk): tt(v("K", 16 * k0, 16 * k0 + 64), v(bk, 0, 64), v("X", 16 * k0, 16 * k0 + 64), Op.add)
 
-        gs(0, 2)
-        if t > 0:
-            act(v("crem"), ind(v("W2"), v("LU", 48, 64)), Fn.Identity)
-        df(0, 2, "B3")
         mm(v("B0", 0, 256), I, v("brep", 0, 256), True, False)
         mm(v("B0", 0, 256), v("NP", 128 * e, 128 * e + 128), v("crem"), False, True)
-        if t == 0:
-            act(v("rl"), v("B0", 0, 256), Fn.Relu)
-        gs(2, 4)
-        if t > 0:
-            act(v("rl"), v("B0", 0, 256), Fn.Relu)
-        df(2, 4, "B4")
+        gs(0, 2)
+        act(v("rl"), v("B0", 0, 256), Fn.Relu)
+        df(0, 2, "B3")
         listify(v("B2", 0, 16), "Big", 0, "rl", 0, 256)
+        gs(2, 4)
+        df(2, 4, "B4")
         sg(0, 2, "B3"); sg(2, 4, "B4")
         gv(14, 16); gv(12, 14); gv(10, 12)
-        ts(v("idle"), v("B2", 0, 16), 0.5, Op.is_lt)
+        ts(v("idle"), v("B2", 0, 16), 0.5, Op.is_lt, 2.0 ** 99, Op.mult)
+        cp(v("Xf"), v("X", 64, 128))
+        ts(v("pen"), ind(v("idle"), v("ex", 0, 4)), 2.0 ** -78, Op.mult)
         score(12, "B5")
         gs(4, 6)
         score(0, "B6")
         df(4, 6, "B3")
-        key(12, "B5"); gv(8, 10)
-        ts(v("pen"), ind(v("idle"), v("ex", 0, 4)), float(1 << 21), Op.mult)
+        gv(8, 10)
         score(8, "B7"); sg(4, 6, "B3")
+        key(12, "B5")
         gv(6, 8); score(4, "B5")
         mm(v("B3", 0, 256), I, v("thr"), True, False)
         key(0, "B6")
         key(8, "B7")
         tt(v("R", 0, 64), v("K", 0, 64), v("K", 192, 256), Op.min)
-        tt(v("R", 64, 128), v("R", 0, 64), v("K", 128, 192), Op.min)
+        tt(v("R", 64, 96), v("K", 128, 160), v("K", 160, 192), Op.min)
+        tt(v("R", 96, 128), v("R", 0, 32), v("R", 32, 64), Op.min)
         tt(v("R", 128, 160), v("R", 64, 96), v("R", 96, 128), Op.min)
-        key(4, "B5")
-        tt(v("R", 128, 160), v("R", 128, 160), v("pen", 0, 32), Op.add)
-        tt(v("R", 160, 192), v("K", 64, 96), v("K", 96, 128), Op.min)
-        tt(v("R", 192, 224), v("R", 160, 192), v("R", 128, 160), Op.min)
+        tt(v("R", 160, 192), v("B5", 0, 32), v("R", 128, 160), Op.min)
+        tt(v("R", 192, 224), v("B5", 32, 64), v("R", 160, 192), Op.min)
         tt(v("ki", 0, 16), v("R", 192, 208), v("R", 208, 224), Op.min)
         ts(v("ki", 16, 32), v("ki", 0, 16), 0x3007FF, Op.bitwise_and)
         ts(v("eu"), v("ki", 16, 32), float(W), Op.min)
@@ -382,6 +385,7 @@ def rank_program(g, core, T, topo):
             act(v("base", 16, 32), v("TRf", 16 * t + 16, 16 * t + 32), Fn.Identity)
             act(v("base", 32, 48), v("TRf", 16 * t + 16, 16 * t + 32), Fn.Identity)
         ts(v("ef"), v("ki", 16, 32), float(W), Op.min)
+        mm(v("B4", 0, 16), v("If"), src, True, False)
         cp(v("D"), ind(v("xi"), v("eu")))
         act(v("Df", 0, 256 - 16 * MS), ind(v("xi"), v("eu", MS, 16)), Fn.Identity)
         eq = lambda m: v("EQ", 272 * m, 256 * m + 256)
@@ -393,33 +397,31 @@ def rank_program(g, core, T, topo):
         for m in range(MS):
             ts(eq(m), v("D", 16 * m, 256), col("ef", m), Op.is_equal, col("wl", m), Op.mult)
             mm(v("B3", 16 * m, 256), v("BR", 0, 128), eq(m), False, False)
-        ts(v("EQ", 4096, 4352), v("D"), float(W), Op.is_equal, 1e29, Op.mult)
         for m in range(MS, 16):
-            mm(v("B3", 16 * m, 256), v("BR", 0, 128), eq(m), False, False)
-        mm(v("B3", 0, 256), v("BR", 0, 128), v("EQ", 4096, 4352), False, True)
+            mm(v("B3", 16 * m, 256), v("BR", 0, 128), eq(m), False, m == 15)
+        ts(v("vt", 0, n), ind(v("ef"), v("ex", 0, n // 16)), float(W), Op.is_equal, -4e29, Op.mult)
         tt(v("dif", 0, 16), v("ef"), v("base", 0, 16), Op.subtract)
         if not last:
             tt(v("dif", 16, 32), v("ef"), v("base", 16, 32), Op.subtract)
             tt(v("dif", 32, 48), v("bq"), v("base", 32, 48), Op.subtract)
-        n = 16 if last else 64
         lf = 64 * (t % 2)
+        tt(v("vs"), v("vt", 0, 16), v("idle"), Op.add)
         scan(v("sc"), v("rst"), v("B3", 0, 256), 0.0, Op.max, Op.min)
-        tt(v("stay"), ind(v("sc"), v("ex15", 0, 1)), v("idle"), Op.is_ge)
-        mm(v("B1", 16, 32), v("RB", 128 * e, 128 * e + 128), v("stay"), True, True)
+        tt(v("stay"), ind(v("sc"), v("ex15", 0, 1)), v("vs"), Op.is_ge)
+        mm(v("B4", 0, 16), v("RB", 128 * e, 128 * e + 128), v("stay"), False, True)
         mm(v("B6", 0, 256), v("BR", 128 * e, 128 * e + 128), v("prod", 256 * (t % 2), 256 * (t % 2) + 256), True, False)
         mm(v("B6", 0, 256), I, v("c512"), False, False)
-        ts(v("land", 0, n), ind(v("sc"), v("ex15", 0, n // 16)), 0.0, Op.is_lt)
-        tt(v("o1f"), v("B1", 16, 32), src, Op.add)
+        tt(v("land", 0, n), ind(v("sc"), v("ex15", 0, n // 16)), v("vt", 0, n), Op.is_lt)
         tt(v("lm", 0, n), v("land", 0, n), v("dif", 0, n), Op.mult)
-        cp(v("o1"), v("o1f"))
+        cp(v("o1"), v("B4", 0, 16))
         tt(v("LF", lf, lf + n), v("lm", 0, n), v("base", 0, n), Op.add)
         cp(ind(Sw, v("o1")), v("crem"))
         cp(v("LU", 0, n), v("LF", lf, lf + n))
         cp(v("W2", 0, 256), ind(Sg, v("eu")))
+        ts(v("em"), v("W2", 0, 256), 256.0, Op.is_ge)
         if not last:
             act(v("val"), ind(Sg, v("LU", 32, 48)), Fn.Identity)
             act(v("ne"), v("val"), Fn.Sign, 256.0, -1.0)
-        ts(v("em"), v("W2", 0, 256), 256.0, Op.is_ge)
         mm(v("B6", 0, 256), v("F"), v("em"), False, True)
         if not last:
             tops_a(t + 1)
@@ -443,14 +445,17 @@ def rank_program(g, core, T, topo):
         if r in far:
             fused([(hp[(r, h)], e_all[8 * h:8 * h + 8], tile("yo", r, h), T.hY[:], "hY") for h in range(2)])
         elif r == near:
-            fused([(nc_, e_off[4 * h:4 * h + 4], tile("yo", r, h), T.aY[2 * me + h], "gY%d" % (2 * me + h)) for h in range(2)])
+            fused([(nc_, e_off, v("yo", 640 * r, 640 * r + 640), T.aN[:], "gY%d" % (2 * me))])
         else:
             for h in range(2):
                 dma("S", home(me, h), tile("yo", me, h), "st")
-    for r in far + [near]:
+    for r in far[::-1]:
         for h in range(2):
-            arrive([slot("aY", 2 * r + h)], "gY%d" % (2 * r + h), 4 if r == near else n_off)
-            dma("Y" if h == 0 else "S", home(r, h), slot("aY", 2 * r + h), "st")
+            arrive([slot("aY", 2 * r + h)], "gY%d" % (2 * r + h), n_off)
+            dma("Y", home(r, h), slot("aY", 2 * r + h), "st")
+    arrive([v("aN")], "gY%d" % (2 * near), n_off)
+    for h in range(2):
+        dma("S", home(near, h), v("aN", 320 * h, 320 * h + 320), "st")
     _emit(g, T, ops, queue)
 
 

@@ -1,10 +1,11 @@
 from concourse.bass import DstId, RemoteDMATransfer
 from concourse.mybir import AluOpType as Op, AxisListType, ActivationFunctionType as Fn
 
-V, W, SP, DUM, WIN = 2560, 2048, 2560, 2816, 5376
+V, W, SB, DUM, WIN, BIG = 2560, 2048, 256, 2560, 5376, 4096.0
 STEP = (1, 2, 3, 1)
-MS = 12
-NS = 6
+MS, MX = 10, 12
+LA, LB = 9, 4
+CS = 96
 
 
 def _sb(n, d):
@@ -13,26 +14,26 @@ def _sb(n, d):
 
 SCRATCH = {}
 for _d, _l in (("b", dict(S=WIN, pin=2560, yo=2560, zt=2560, I=128, nI=128, tm=128, tn=128, Big=576, BigW=144, BR=512, NP=512, RB=512,
-                          D512=128, D256=128, F=128, SI=896, SO=528, kk=256, c512=256, thr=256, stay=16, pen=64, dS=2048, cmp=4096,
-                          brep=512, EQ=4096, W2=512, val=256, ne=256, em=256, prod=512, crem=256, rl=256, nc=256)),
-               ("f", dict(If=128, vt=64, vs=16, Xf=64, TRf=64, xi=2064, xs=528, xg=128, xm=256, cf=16, cd=32, wl=16, wn=16, rst=256,
-                          wrep=256, msel=256, t1=256, t2=256, base=64, dif=64, land=64, lm=64, LF=128, b97=16, bq=16, idle=16, K=256,
-                          R=256, ef=16, Df=256, ab=512, sc=256)),
+                          DT=128, F=128, SI=896, SO=528, kk=256, c256=320, thr=256, nl=16, ask=16, bl=16, idle=16, cst=80,
+                          BI=128, BRw=128 * (16 - MS), dS=2048, cmp=4096, brep=512, EQ=4096, ES=1024, W2=512, val=256, em=256,
+                          prod=512, crem=256, rl=256, nc=256)),
+               ("f", dict(If=128, vt=16, Xf=64, TRf=64, xi=2064, xs=528, xg=128, xm=256, cf=16, cd=32, wl=16, rst=256,
+                          wrep=256, msel=256, t1=256, t2=256, base=80, lm=16, LF=80, b97=16, K=256,
+                          R=256, ef=16, Df=256, ab=1024, sc=256)),
                ("i", dict(P=1024, TR=64, p4=4, ci=16, X=256, XA=256, ki=32)),
-               ("u", dict(ex=16, ex15=4, LU=64, o1=16, O=256, eu=16, D=256))):
+               ("u", dict(ex=16, ex15=4, LU=80, O=256, eu=16, D=256))):
     for _n, _w in _l.items():
         SCRATCH[_n] = _sb(_w, _d)
-for _n, _w in (("T", 8), ("A", 32), ("B", 96)):
-    SCRATCH.update({"d" + _n: ("dram", [8, 128, _w], "int32"), "a" + _n: ("dram", [8, 128, _w], "int32"), "h" + _n: ("dram", [128, _w], "int32")})
+for _n, _k, _w in (("T", 8, 8), ("A", 4, 64), ("B", 4, 192)):
+    SCRATCH.update({"d" + _n: ("dram", [_k, 128, _w], "int32"), "a" + _n: ("dram", [_k, 128, _w], "int32"), "h" + _n: ("dram", [128, _w], "int32")})
 SCRATCH.update({
-    "dD": ("dram", [8, 128, 320], "bfloat16"), "aY": ("dram", [8, 128, 320], "bfloat16"),
-    "dN": ("dram", [128, 640], "bfloat16"), "aN": ("dram", [128, 640], "bfloat16"),
+    "dD": ("dram", [8, 128, 320], "bfloat16"), "aY": ("dram", [8, 128, 320], "bfloat16"), "aN": ("dram", [128, 640], "bfloat16"),
     "hD": ("dram", [128, 320], "bfloat16"), "hY": ("dram", [128, 320], "bfloat16"),
 })
 for _b in range(8):
     SCRATCH["B%d" % _b] = ("psum", [128, 512], "float32")
 
-SEMAPHORES = (["cV", "cS", "cT", "cG", "lA", "lC", "lX", "lD", "lB", "lS", "lM", "lN", "lT", "s2", "st", "sent", "gA", "gB", "gT", "hT",
+SEMAPHORES = (["cV", "cS", "cT", "cG", "lA", "lC", "lX", "lB", "lS", "lM", "lN", "lT", "s2", "st", "sent", "gA", "gB", "gT", "hT",
                "hA", "hB", "hD", "hY"] + ["gD%d" % i for i in range(8)] + ["gY%d" % i for i in range(8)])
 
 
@@ -69,8 +70,9 @@ def _helper_program(g, core, T, topo):
     m = topo.mask(core, dst)
     n = len(topo.engines(core, dst))
     k = 2 * r + h
-    steps = [("hT", 2, T.hT[:], T.aT[k], "gT"), ("hD", 4, T.hD[:], T.pin[:, 320 * k:320 * k + 320], "gD%d" % k),
-             ("hA", 2, T.hA[:], T.aA[k], "gA"), ("hB", 2, T.hB[:], T.aB[k], "gB"), ("hY", 8, T.hY[:], T.aY[k], "gY%d" % k)]
+    x = "AB"[h]
+    steps = [("hT", 1, T.hT[:], T.aT[k], "gT"), ("hD", 2, T.hD[:], T.pin[:, 320 * k:320 * k + 320], "gD%d" % k),
+             ("h" + x, 4, T["h" + x][:], T["a" + x][r], "g" + x), ("hY", len(topo.engines(home[0], core)), T.hY[:], T.aY[k], "gY%d" % k)]
     for s, cnt, src, out, rs in steps:
         g.wait_ge(T.sem[s], cnt)
         g.remote_dma(out, src, T.sem[rs], T.sem.sent, pid, rid, m)
@@ -107,7 +109,7 @@ def rank_program(g, core, T, topo):
         wr, rd = [], []
         for o in outs:
             if len(o) == 4:
-                wr += o[2]
+                wr += [x[:5] + (False,) for x in o[2]]
                 rd += o[3]
             else:
                 wr += o[1]
@@ -158,41 +160,40 @@ def rank_program(g, core, T, topo):
     hk = [(q, h) for q in far for h in range(2)]
     others = far + [near]
     mine = (32 * me, 32 * me + 32)
-    days = lambda q, h: ext(T.days[32 * q:32 * q + 32, 1280 * h:1280 * h + 1280])
+    days = lambda q, h: T.days[32 * q:32 * q + 32, 1280 * h:1280 * h + 1280]
+    rows = lambda x, q: x[32 * q:32 * q + 32, :]
     tile = lambda name, r, h: v(name, 640 * r + 320 * h, 640 * r + 320 * h + 320)
 
-    def yards(x):
-        fused([(hp[k], e_on[2 * n:2 * n + 2], slot("d" + x, 2 * k[0] + k[1]), T["h" + x][:], "h" + x) for n, k in enumerate(hk)]
-              + [(nc_, e_off[4 * h:4 * h + 4], slot("d" + x, 2 * near + h), T["a" + x][2 * me + h], "g" + x) for h in range(2)])
+    def numbers(x, h):
+        fused([(hp[(q, h)], e_on[4 * n:4 * n + 4], slot("d" + x, q), T["h" + x][:], "h" + x) for n, q in enumerate(far)]
+              + [(nc_, e_off, slot("d" + x, near), T["a" + x][me], "g" + x)])
     dma("S", slot("dT", 0, 8), ext(T.trucks[:, :]), "lC")
-    for q, h in hk:
-        dma("Y", slot("dD", 2 * q + h), days(q, h), "lX")
-    for h in range(2):
-        dma("Y", v("dN", 320 * h, 320 * h + 320), days(near, h), "lD")
-    dma("Y", slot("dA", 0, 8), ext(T.cand[:, 0:256]), "lA")
-    for h in range(2):
-        dma("Y", tile("pin", me, h), days(me, h), "lS")
+    for q in others:
+        for h in range(2):
+            dma("Y", slot("dD", 2 * q + h), ext(days(q, h)), "lX")
+    dma("Y", slot("dA", 0, 4), ext(T.cand[:, 0:256]), "lA")
+    dma("Y", v("pin", 640 * me, 640 * me + 640), ext(rows(T.days, me)), "lS")
     sent_far = (None, [("gate", 0, 1, 0, 128, True)])
 
     iota(v("p4"), [[32, 4]], 0, 1, False)
-    iota(v("xs"), [[1, 528]], 0, 0)
+    iota(v("xs", 0, 256), [[1, 256]], 0, 0)
     iota(v("xg"), [[16, 8], [0, 16]], 0, 0)
-    yards("T")
-    fused([(hp[k], e_all[4 * n:4 * n + 4], slot("dD", 2 * k[0] + k[1]), T.hD[:], "hD") for n, k in enumerate(hk)], "s2", [sent_far])
-    fused([(nc_, e_off, (T.dN[:], v("dN")[1]), T.pin[:, 640 * me:640 * me + 640], "gD%d" % (2 * me))])
-    yards("A")
-    dma("Y", v("TR", 0, 64, p=mine), (T.trucks[mine[0]:mine[1], :], sent_far[1]), "lT")
-    dma("Y", v("P", 0, 1024, p=mine), ext(T.cand[mine[0]:mine[1], :]), "lM")
+    fused([(hp[k], e_on[n:n + 1], slot("dT", 2 * k[0] + k[1]), T.hT[:], "hT") for n, k in enumerate(hk)]
+          + [(nc_, e_off[2 * h:2 * h + 1], slot("dT", 2 * near + h), T.aT[2 * me + h], "gT") for h in range(2)])
+    fused([(hp[k], e_on[n::4], slot("dD", 2 * k[0] + k[1]), T.hD[:], "hD") for n, k in enumerate(hk)]
+          + [(nc_, e_off[4 * h:4 * h + 4], slot("dD", 2 * near + h), tile("pin", me, h)[0], "gD%d" % (2 * me)) for h in range(2)], "s2", [sent_far])
+    numbers("A", 0)
+    dma("Y", v("TR", 0, 64, p=mine), (rows(T.trucks, me), sent_far[1]), "lT")
+    dma("Y", v("P", 0, 1024, p=mine), ext(rows(T.cand, me)), "lM")
     for q in others:
-        dma("Y", slot("dB", 2 * q, 2), ext(T.cand[32 * q:32 * q + 32, 256:1024]), "lB")
-    iota(v("xm"), [[0, 16], [1, 16]], 0, 0)
-    iota(v("kk"), [[2048, 16], [0, 16]], 0, 0)
+        dma("Y", slot("dB", q), ext(T.cand[32 * q:32 * q + 32, 256:1024]), "lB")
     iota(v("xi"), [[1, 2064]], 0, 0)
-    yards("B")
-    iota(v("S", DUM, WIN), [[0, WIN - DUM]], 0, 0)
+    numbers("B", 1)
+    iota(v("S", SB + DUM, WIN), [[0, WIN - SB - DUM]], 0, 0)
 
-    for x in "TAB":
-        arrive([slot("a" + x, 2 * r, 2) for r in others], "g" + x, 8 + 4 * n_off)
+    arrive([slot("aT", 2 * r, 2) for r in others], "gT", 2 + 4 * n_off)
+    for x in "AB":
+        arrive([slot("a" + x, r) for r in others], "g" + x, 3 * n_off)
     arrive([tile("pin", near, 0), tile("pin", near, 1)], "gD%d" % (2 * near), n_off)
     for r in far:
         for h in range(2):
@@ -200,9 +201,9 @@ def rank_program(g, core, T, topo):
     for r in others:
         dma("Y", v("TR", 0, 64, p=(32 * r, 32 * r + 32)), slot("aT", 2 * r, 2), "lT")
     for r in others:
-        dma("Y", v("P", 0, 256, p=(32 * r, 32 * r + 32)), slot("aA", 2 * r, 2), "lM")
+        dma("Y", v("P", 0, 256, p=(32 * r, 32 * r + 32)), slot("aA", r), "lM")
     for r in others:
-        dma("Y", v("P", 256, 1024, p=(32 * r, 32 * r + 32)), slot("aB", 2 * r, 2), "lN")
+        dma("Y", v("P", 256, 1024, p=(32 * r, 32 * r + 32)), slot("aB", r), "lN")
 
     col = lambda name, j: v(name, j, j + 1)
     ts(v("ci", 0, 4), v("p4"), 127, Op.bitwise_and)
@@ -213,7 +214,7 @@ def rank_program(g, core, T, topo):
     cp(v("cf", 0, 11), v("ci", 0, 11))
     pf, rf = col("cf", 0), col("cf", 8)
     ts(col("cd", 4), col("cf", 10), 96.0, Op.add)
-    ts(v("cd", 12, 16), v("xs", 0, 4), col("cf", 9), Op.is_equal)
+    ts(v("cd", 12, 16), v("xs", 0, 4), col("cf", 9), Op.is_equal, -1.0, Op.mult)
     for j in range(4):
         ts(v("SI", 224 * j, 224 * j + 224), v("xs", 0, 224), col("cd", 4), Op.is_equal, col("cd", 12 + j), Op.mult)
     ts(v("cd", 0, 4), v("cf", 4, 8), 15.0, Op.add)
@@ -221,14 +222,14 @@ def rank_program(g, core, T, topo):
     ts(col("cd", 11), rf, 15.0, Op.is_equal, 256.0, Op.mult)
     ts(col("cd", 7), pf, -1.0, Op.add)
     ts(col("cd", 8), pf, 1.0, Op.add)
-    ts(col("cd", 9), rf, 0.0, Op.not_equal, -512.0, Op.mult)
+    ts(col("cd", 9), rf, 0.0, Op.not_equal, -256.0, Op.mult)
     ts(col("cd", 10), rf, 15.0, Op.not_equal, 512.0, Op.mult)
     ts(col("cd", 16), rf, 0.0, Op.is_equal)
-    ts(col("cd", 17), rf, 0.0, Op.not_equal, 256.0, Op.mult)
     ts(col("cd", 18), rf, 16.0, Op.mult, 15.0, Op.add)
     ts(col("cd", 6), col("cd", 11), 3840.0, Op.mult, 65536.0, Op.add)
     act(col("cd", 24), rf, Fn.Sigmoid, 580.0, -40.0)
     ts(v("I"), v("xs", 0, 128), pf, Op.is_equal)
+    ms(v("c256"), 256.0)
     ts(v("If"), v("xs", 0, 128), pf, Op.is_equal)
     ts(v("nI"), v("xs", 0, 128), pf, Op.is_equal, -1.0, Op.mult)
     ts(v("tm"), v("xs", 0, 128), pf, Op.is_equal, 512.0, Op.mult)
@@ -237,25 +238,31 @@ def rank_program(g, core, T, topo):
     for e in range(4):
         ts(v("Big", 144 * e, 144 * e + 144), v("xs", 0, 144), col("cd", e), Op.is_equal)
         ts(v("BR", 128 * e, 128 * e + 128), v("xg"), col("cf", 4 + e), Op.is_equal)
-    tt(v("D512"), v("tm"), v("tn"), Op.add)
-    tt(v("F"), v("F"), v("tm"), Op.subtract)
+    tt(v("DT"), v("I"), v("tn"), Op.add)
+    tt(v("F"), v("tm"), v("F"), Op.subtract)
     for e in range(1, 4):
-        ts(v("NP", 128 * e, 128 * e + 128), v("xs", 0, 128), col("cf", e), Op.is_equal, -1.0, Op.mult)
+        ts(v("NP", 128 * e, 128 * e + 128), v("xs", 0, 128), col("cf", e), Op.is_equal)
         ts(v("RB", 128 * e, 128 * e + 128), v("xs", 0, 128), col("cf", 4 - e), Op.is_equal, float(DUM), Op.mult)
-    ts(v("D256"), v("D512"), 0.5, Op.mult)
     ts(v("BigW"), v("xs", 0, 144), col("cd", 0), Op.is_equal, col("cd", 6), Op.mult)
-    ts(v("S", SP, DUM), v("xs", 0, 256), col("cd", 16), Op.mult, col("cd", 17), Op.add)
+    ts(v("S", 0, SB), v("xs", 0, 256), col("cd", 16), Op.mult)
     ts(v("ex"), v("xs", 0, 16), 0.0, Op.mult, rf, Op.add)
     ts(v("ex15"), v("xs", 0, 4), 0.0, Op.mult, col("cd", 18), Op.add)
-    ts(v("lm", 0, 16), v("xs", 0, 16), 16.0, Op.mult, rf, Op.add)
-    ms(v("c512"), 512.0)
+    ts(v("lm"), v("xs", 0, 16), 16.0, Op.mult, rf, Op.add)
     ms(v("t1"), 1.0 / 1.8)
     ms(v("t2"), 0.0)
-    ms(v("dif", 48, 64), -256.0)
-    ts(v("base", 0, 16), v("lm", 0, 16), float(DUM), Op.add)
-    ts(v("base", 48, 64), v("lm", 0, 16), 256.0, Op.add)
+    ts(v("base", 16, 32), v("lm"), float(DUM), Op.add)
+    ts(v("base", 64, 80), v("lm"), 256.0, Op.add)
+    ms(v("cst", 0, 16), -float(DUM))
+    ms(v("cst", 16, 64), 0.0)
+    cp(v("cst", 64, 80), v("lm"))
+    ts(v("BI"), v("I"), BIG, Op.mult)
     scan(v("wrep"), v("t1"), v("t2"), 1.8e29, Op.mult, Op.add)
-    ts(v("SO"), v("xs"), col("cd", 5), Op.is_equal)
+    for a, b in ((256, 512), (512, 528)):
+        act(v("xs", a, b), v("xs", 0, b - a), Fn.Identity, float(a))
+    for a in (0, 128):
+        tt(v("xm", a, a + 128), v("xs", 0, 128), v("xg"), Op.subtract)
+        act(v("kk", a, a + 128), v("xg"), Fn.Identity, 128.0 * a, 128.0)
+    ts(v("SO"), v("xs"), col("cd", 5), Op.is_equal, -1.0, Op.mult)
     ts(v("msel"), v("xm"), rf, Op.is_equal)
     ts(v("rst"), v("xm"), 0.0, Op.not_equal, -9e29, Op.mult)
     tt(v("t1"), v("wrep"), v("msel"), Op.mult)
@@ -263,172 +270,185 @@ def rank_program(g, core, T, topo):
     ts(v("thr"), v("t1"), -2.5, Op.mult)
     ts(col("cd", 20), col("cd", 19), 1e-29, Op.mult)
     ts(v("wl"), v("wrep", 0, 256, 16), col("cd", 20), Op.mult)
-    ts(v("wn"), v("wl"), -1.0, Op.mult)
+    for m in range(MS, 16):
+        ts(v("BRw", 128 * (m - MS), 128 * (m - MS) + 128), v("BR", 0, 128), col("wl", m), Op.mult)
 
-    def sel_in(r, h, j, st, en):
-        mm(v("B%d" % (4 * h + j), 0, 320), v("SI", 224 * j + 96 - 32 * r, 224 * j + 224 - 32 * r), tile("pin", r, h), st, en)
+    def fill(b): mm(v("B%d" % b, 0, 320), v("I"), v("c256"), True, False)
+
+    def sel_in(r, b, en):
+        j, x = (b % 4, b // 4) if r != me else (b // 2, b % 2)
+        mm(v("B%d" % b, 0, 320), v("SI", 224 * j + 96 - 32 * r, 224 * j + 224 - 32 * r), tile("pin", r, x), False, en)
+    for b in range(8):
+        fill(b)
     for r in (me, near):
-        for h in range(2):
-            for j in range(4):
-                sel_in(r, h, j, r == me, False)
-    for h in range(2):
-        for j in range(4):
-            sel_in(far[0], h, j, False, False)
-            sel_in(far[1], h, j, False, True)
-            b = 4 * h + j
-            z = v("zt", 320 * b, 320 * b + 320)
-            act(z, v("B%d" % b, 0, 320), Fn.Relu, 256.0, -256.0)
-            if b == 7:
-                cp(v("LU", 32, 48), v("TR", 0, 16))
-            tt(v("S", 320 * b, 320 * b + 320), v("B%d" % b, 0, 320), z, Op.add)
+        for b in range(8):
+            sel_in(r, b, False)
+    for b in range(8):
+        sel_in(far[0], b, False)
+        sel_in(far[1], b, True)
+        z = v("zt", 320 * b, 320 * b + 320)
+        act(z, v("B%d" % b, 0, 320), Fn.Relu, 65536.0, -256.0)
+        if b == 7:
+            ts(v("LU", 48, 64), v("TR", 0, 16), float(SB), Op.add)
+        tt(v("S", SB + 320 * b, SB + 320 * b + 320), v("B%d" % b, 0, 320), z, Op.min)
 
     I, nI = v("I"), v("nI")
-    Sg, Sw = v("S", 0, DUM), v("S", 0, WIN)
+    Sv, Sg, Sw = v("S", 0, SB + V), v("S", SB, SB + V), v("S", SB, WIN)
+    prod = lambda t: v("prod", 256 * (t % 2), 256 * (t % 2) + 256)
 
     def listify(out, big, c0, src, a, b, first=True, end=True):
         for r in range(16):
             mm(out, v(big, c0 + 15 - r, c0 + 143 - r), v(src, a + r, b, 16), first and r == 0, end and r == 15)
 
-    def tops_a(t):
-        pr = v("prod", 256 * (t % 2), 256 * (t % 2) + 256)
-        mm(v("B0", 0, 256), I, v("val"), True, False)
-        mm(v("B0", 0, 256), v("D512"), v("ne"), False, True)
-        act(pr, v("B0", 0, 256), Fn.Relu, -512.0, 1.0)
-        mm(v("B7", 0, 256), I, v("val"), True, False)
-        mm(v("B7", 0, 256), v("D256"), v("ne"), False, False)
-        mm(v("B7", 0, 256), nI, pr, False, True)
-        act(v("crem") if t == 0 else v("W2", 256, 512), v("B7", 0, 256), Fn.Identity)
-
-    def tops_b(t):
+    def tops(t):
         e = STEP[t]
         a = 256 * (t % 2)
-        pr = v("prod", a, a + 256)
         br = v("BR", 128 * e, 128 * e + 128)
         listify(v("B1", 0, 16), "Big", 144 * e, "prod", a, a + 256)
-        mm(v("B2", 0, 256), br, pr, True, True)
-        mm(v("B2", 256, 512), br, pr, True, True)
-        act(v("b97"), v("B1", 0, 16), Fn.Identity, 0.0, 97.0)
-        if t > 0:
-            act(v("crem"), ind(v("W2"), v("LU", 48, 64)), Fn.Identity)
-        act(v("brep"), v("B2"), Fn.Identity, col("cd", 11), col("cd", 24))
+        mm(v("B2", 0, 256), br, prod(t), True, True)
+        mm(v("B2", 256, 512), br, prod(t), True, True)
+        mm(v("B7", 0, 256), I, v("val"), True, False)
+        mm(v("B7", 0, 256), nI, prod(t), False, True)
+        act(v("b97"), v("B1", 0, 16), Fn.Identity, 97.0 * 256, -97.0)
+        act(v("brep"), v("B2"), Fn.Identity, 0.0, col("cd", 24))
+        if t < 3:
+            act(v("bl"), v("B1", 0, 16), Fn.Identity)
+        act(v("crem") if t == 0 else v("W2", 256, 512), v("B7", 0, 256), Fn.Identity)
 
-    act(v("val"), ind(Sg, v("LU", 32, 48)), Fn.Identity)
-    ts(v("ne"), ind(Sg, v("LU", 32, 48)), 256.0, Op.is_lt)
+    act(v("val"), ind(Sv, v("LU", 48, 64)), Fn.Identity)
     cp(v("TRf"), v("TR"))
-    tops_a(0)
-    tops_b(0)
+    mm(v("B0", 0, 256), v("DT"), v("val"), True, True)
+    ts(prod(0), v("B0", 0, 256), 0.0, Op.max)
+    tops(0)
     for t in range(4):
         e, last = STEP[t], t == 3
-        n = 16 if last else 64
-        src = v("TRf", 0, 16) if t == 0 else v("LF", 64 * ((t - 1) % 2) + 16, 64 * ((t - 1) % 2) + 32)
-        parts = ((0, 16 * NS), (16 * NS, 256))
-        for a, b in parts:
-            tt(v("X", a, b), ind(v("b97"), v("ex", 0, (b - a) // 16)), v("P", 256 * t + a, 256 * t + b), Op.add)
-        for a, b in parts:
-            ts(v("XA", a, b), v("X", a, b), W - 1, Op.bitwise_and)
-        for a, b in ((0, 96), (192, 256), (96, 192)):
-            cp(v("O", a, b), v("XA", a, b))
-
-        def gv(k0, k1): tt(v("cmp", 256 * k0, 256 * k1), ind(Sg, v("O", 16 * k0, 16 * k1)), v("brep", 0, 256 * (k1 - k0)), Op.is_lt)
-        def gs(k0, k1): act(v("dS", 256 * k0, 256 * k1), ind(Sg, v("O", 16 * k0, 16 * k1)), Fn.Identity)
-        def df(k0, k1, bk):
-            o = v(bk, 0, 256 * (k1 - k0))
-            mm(o, I, v("brep", 0, 256 * (k1 - k0)), True, False)
-            mm(o, nI, v("dS", 256 * k0, 256 * k1), False, True)
-        def sg(k0, k1, bk): act(v("cmp", 256 * k0, 256 * k1), v(bk, 0, 256 * (k1 - k0)), Fn.Sigmoid, -20.0, 40.0)
-        def score(k0, bk):
-            mm(v(bk, 0, 64), I, v("kk", 16 * k0, 16 * k0 + 64), True, False)
-            if k0 != 12:
-                mm(v(bk, 0, 64), I, v("pen"), False, False)
-            if k0 == 4:
+        n = 32 if last else 80
+        src = v("TRf", 0, 16) if t == 0 else v("LF", 32, 48)
+        def xo(a, b): tt(v("X", a, b), ind(v("b97"), v("ex", 0, (b - a) // 16)), v("P", 256 * t + a, 256 * t + b), Op.add)
+        def xa(a, b): ts(v("XA", a, b), v("X", a, b), W - 1, Op.bitwise_and)
+        def xu(a, b): cp(v("O", a, b), v("XA", a, b))
+        rep = lambda a, b: v("brep", 16 * a % 256, 16 * a % 256 + 16 * (b - a))
+        def gv(a, b): tt(v("cmp", 16 * a, 16 * b), ind(Sg, v("O", a, b)), rep(a, b), Op.is_gt)
+        def gs(a, b): act(v("dS", 16 * a, 16 * b), ind(Sg, v("O", a, b)), Fn.Identity)
+        def df(a, b, bk):
+            o = v(bk, 0, 16 * (b - a))
+            mm(o, nI, rep(a, b), True, False)
+            mm(o, I, v("dS", 16 * a, 16 * b), False, True)
+        def sg(a, b, bk): act(v("cmp", 16 * a, 16 * b), v(bk, 0, 16 * (b - a)), Fn.Sigmoid, -20.0, 40.0)
+        def lead(a, bk):
+            mm(v(bk, 0, 64), I, v("kk", a, a + 64), True, False)
+            if a == 64:
                 mm(v(bk, 0, 64), v("If"), v("Xf"), False, False)
-            listify(v(bk, 0, 64), "BigW", 0, "cmp", 256 * k0, 256 * k0 + 1024, False, k0 != 12)
-            if k0 == 12:
-                mm(v(bk, 0, 64), I, v("pen"), False, True)
-        def key(k0, bk): tt(v("K", 16 * k0, 16 * k0 + 64), v(bk, 0, 64), v("X", 16 * k0, 16 * k0 + 64), Op.add)
+        def score(a, bk): listify(v(bk, 0, 64), "BigW", 0, "cmp", 16 * a, 16 * a + 1024, False, True)
+        def key(a, bk): tt(v("K", a, a + 64), v(bk, 0, 64), v("X", a, a + 64), Op.add)
 
-        mm(v("B0", 0, 256), I, v("brep", 0, 256), True, False)
-        mm(v("B0", 0, 256), v("NP", 128 * e, 128 * e + 128), v("crem"), False, True)
-        gs(0, 2)
-        act(v("rl"), v("B0", 0, 256), Fn.Relu)
-        df(0, 2, "B3")
-        listify(v("B2", 0, 16), "Big", 0, "rl", 0, 256)
-        gs(2, 4)
-        df(2, 4, "B4")
-        sg(0, 2, "B3"); sg(2, 4, "B4")
-        gv(14, 16); gv(12, 14); gv(10, 12)
-        ts(v("idle"), v("B2", 0, 16), 0.5, Op.is_lt, 2.0 ** 99, Op.mult)
+        xo(0, 64); xo(192, 256); xa(0, 64); xa(192, 256); xu(0, 64); xu(192, 256); xo(64, 192)
+        gs(0, 32)
+        df(0, 32, "B3")
+        gs(32, 64)
+        for a, bk in ((192, "B5"), (0, "B6"), (128, "B2")):
+            lead(a, bk)
+        df(32, 64, "B4")
+        sg(0, 32, "B3")
+        sg(32, 64, "B4")
+        gv(224, 256); xa(64, 192); gv(192, 224); xu(64, 192)
         cp(v("Xf"), v("X", 64, 128))
-        ts(v("pen"), ind(v("idle"), v("ex", 0, 4)), 2.0 ** -78, Op.mult)
-        score(12, "B5")
-        gs(4, 6)
+        gv(160, 192)
+        score(192, "B5")
+        gs(64, CS)
+        lead(64, "B1")
+        mm(v("B0", 0, 256), nI, v("brep", 0, 256), True, False)
         score(0, "B6")
-        df(4, 6, "B3")
-        gv(8, 10)
-        score(8, "B7"); sg(4, 6, "B3")
-        key(12, "B5")
-        gv(6, 8); score(4, "B5")
+        df(64, CS, "B3")
+        if t > 0:
+            act(v("crem"), ind(v("W2"), v("LU", 64, 80)), Fn.Identity)
+        gv(128, 160)
+        key(192, "B5")
+        score(128, "B2"); sg(64, CS, "B3")
+        gv(CS, 128)
+        rb = v("RB", 128 * e, 128 * e + 128)
+        lst = lambda i: v("B4" if i else "B5", 16 * i, 16 * i + 16)
+        mm(v("B0", 0, 256), v("NP", 128 * e, 128 * e + 128), v("crem"), False, True)
+        score(64, "B1")
+        act(v("rl"), v("B0", 0, 256), Fn.Relu)
+        listify(v("B7", 0, 16), "Big", 0, "rl", 0, 256)
+        act(v("idle"), v("B7", 0, 16), Fn.Relu, BIG, -BIG)
         mm(v("B3", 0, 256), I, v("thr"), True, False)
         key(0, "B6")
-        key(8, "B7")
+        key(128, "B2")
         tt(v("R", 0, 64), v("K", 0, 64), v("K", 192, 256), Op.min)
         tt(v("R", 64, 96), v("K", 128, 160), v("K", 160, 192), Op.min)
         tt(v("R", 96, 128), v("R", 0, 32), v("R", 32, 64), Op.min)
         tt(v("R", 128, 160), v("R", 64, 96), v("R", 96, 128), Op.min)
-        tt(v("R", 160, 192), v("B5", 0, 32), v("R", 128, 160), Op.min)
-        tt(v("R", 192, 224), v("B5", 32, 64), v("R", 160, 192), Op.min)
+        tt(v("R", 160, 192), v("B1", 0, 32), v("R", 128, 160), Op.min)
+        tt(v("R", 192, 224), v("B1", 32, 64), v("R", 160, 192), Op.min)
         tt(v("ki", 0, 16), v("R", 192, 208), v("R", 208, 224), Op.min)
-        ts(v("ki", 16, 32), v("ki", 0, 16), 0x3007FF, Op.bitwise_and)
+        ts(v("ki", 16, 32), v("ki", 0, 16), 0x1007FF, Op.bitwise_and)
         ts(v("eu"), v("ki", 16, 32), float(W), Op.min)
+        tt(v("ef"), v("ki", 16, 32), v("idle"), Op.add)
+        cp(v("D", 128, 256), ind(v("xi"), v("eu", 8, 16)))
+        cp(v("D", 0, 128), ind(v("xi"), v("eu", 0, 8)))
+        mm(lst(0), I, v("cst", 0, 16), True, False)
+        mm(v("B4", 16, n), I, v("cst", 16, n), True, False)
+        mm(lst(0), v("If"), src, False, False)
         if not last:
-            act(v("bq"), v("B1", 0, 16), Fn.Identity, float(SP), 1.0)
-            act(v("base", 16, 32), v("TRf", 16 * t + 16, 16 * t + 32), Fn.Identity)
-            act(v("base", 32, 48), v("TRf", 16 * t + 16, 16 * t + 32), Fn.Identity)
-        ts(v("ef"), v("ki", 16, 32), float(W), Op.min)
-        mm(v("B4", 0, 16), v("If"), src, True, False)
-        cp(v("D"), ind(v("xi"), v("eu")))
-        act(v("Df", 0, 256 - 16 * MS), ind(v("xi"), v("eu", MS, 16)), Fn.Identity)
+            mm(lst(3), I, v("bl"), False, False)
+        mm(v("B6", 0, 256), v("BR", 128 * e, 128 * e + 128), prod(t), True, False)
+        m0 = MS - MS % 2
+        act(v("Df", 0, 256 - 16 * m0), ind(v("xi"), v("eu", m0, 16)), Fn.Identity)
         eq = lambda m: v("EQ", 272 * m, 256 * m + 256)
         pos = lambda m: sum(256 - 16 * x for x in range(MS, m))
-        for m in range(MS, 16):
-            act(v("ab", pos(m), pos(m + 1)), v("Df", 16 * (m - MS), 256 - 16 * MS), Fn.Abs, col("ef", m), -1.0)
-        for m in range(MS, 16):
-            act(eq(m), v("ab", pos(m), pos(m + 1)), Fn.Relu, col("wl", m), col("wn", m))
-        for m in range(MS):
+        for a, b in ((MS, MX), (MX, 16)):
+            for m in range(a, b):
+                act(v("ab", pos(m), pos(m + 1)), v("Df", 16 * (m - m0), 256 - 16 * m0), Fn.Abs, col("ef", m), -1.0)
+            act(v("ES", pos(a), pos(b)), v("ab", pos(a), pos(b)), Fn.Relu, 1.0, -1.0)
+        act(v("ask"), v("B7", 0, 16), Fn.Sign)
+        if not last:
+            act(v("base", 32, 48), v("TRf", 16 * t + 16, 16 * t + 32), Fn.Identity)
+            act(v("base", 48, 64), v("TRf", 16 * t + 16, 16 * t + 32), Fn.Identity, float(SB))
+
+        def late(a, b):
+            for m in range(a, b):
+                mm(v("B3", 16 * m, 256), v("BRw", 128 * (m - MS), 128 * (m - MS) + 128), v("ES", pos(m), pos(m + 1)), False, False)
+        for m in list(range(8, MS)) + list(range(8)):
             ts(eq(m), v("D", 16 * m, 256), col("ef", m), Op.is_equal, col("wl", m), Op.mult)
-            mm(v("B3", 16 * m, 256), v("BR", 0, 128), eq(m), False, False)
-        for m in range(MS, 16):
-            mm(v("B3", 16 * m, 256), v("BR", 0, 128), eq(m), False, m == 15)
-        ts(v("vt", 0, n), ind(v("ef"), v("ex", 0, n // 16)), float(W), Op.is_equal, -4e29, Op.mult)
-        tt(v("dif", 0, 16), v("ef"), v("base", 0, 16), Op.subtract)
-        if not last:
-            tt(v("dif", 16, 32), v("ef"), v("base", 16, 32), Op.subtract)
-            tt(v("dif", 32, 48), v("bq"), v("base", 32, 48), Op.subtract)
-        lf = 64 * (t % 2)
-        tt(v("vs"), v("vt", 0, 16), v("idle"), Op.add)
+            mm(v("B3", 16 * m, 256), v("BR", 0, 128), eq(m), False, m == 7)
+            if m == LA:
+                late(MS, MX)
+            if m == LB:
+                late(MX, 16)
+        mm(lst(0), rb, v("ask"), False, False)
+        for i in range(1, 2 if last else 3):
+            mm(lst(i), v("If"), v("ef"), False, False)
+        ts(v("vt"), v("ef"), float(W), Op.is_ge, -4e29, Op.mult)
         scan(v("sc"), v("rst"), v("B3", 0, 256), 0.0, Op.max, Op.min)
-        tt(v("stay"), ind(v("sc"), v("ex15", 0, 1)), v("vs"), Op.is_ge)
-        mm(v("B4", 0, 16), v("RB", 128 * e, 128 * e + 128), v("stay"), False, True)
-        mm(v("B6", 0, 256), v("BR", 128 * e, 128 * e + 128), v("prod", 256 * (t % 2), 256 * (t % 2) + 256), True, False)
-        mm(v("B6", 0, 256), I, v("c512"), False, False)
-        tt(v("land", 0, n), ind(v("sc"), v("ex15", 0, n // 16)), v("vt", 0, n), Op.is_lt)
-        tt(v("lm", 0, n), v("land", 0, n), v("dif", 0, n), Op.mult)
-        cp(v("o1"), v("B4", 0, 16))
-        tt(v("LF", lf, lf + n), v("lm", 0, n), v("base", 0, n), Op.add)
-        cp(ind(Sw, v("o1")), v("crem"))
-        cp(v("LU", 0, n), v("LF", lf, lf + n))
-        cp(v("W2", 0, 256), ind(Sg, v("eu")))
-        ts(v("em"), v("W2", 0, 256), 256.0, Op.is_ge)
-        if not last:
-            act(v("val"), ind(Sg, v("LU", 32, 48)), Fn.Identity)
-            act(v("ne"), v("val"), Fn.Sign, 256.0, -1.0)
+        tt(v("nl"), ind(v("sc"), v("ex15", 0, 1)), v("vt"), Op.is_ge)
+        mm(lst(0), rb, v("nl"), False, True)
+        for i in range(1, n // 16):
+            mm(lst(i), v("BI"), v("nl"), False, i == n // 16 - 1)
+        cp(v("LU", 0, 16), lst(0))
+        tt(v("LF", 16, n), v("B4", 16, n), v("base", 16, n), Op.min)
+        cp(ind(Sw, v("LU", 0, 16)), v("crem"))
+        cp(v("LU", 16, n), v("LF", 16, n))
+        ts(v("em"), ind(Sg, v("eu")), 0.5, Op.is_lt)
+        if last:
+            act(v("W2", 0, 256), ind(Sg, v("eu")), Fn.Identity)
+            for b in (0, 1, 2, 3, 4, 5, 7):
+                fill(b)
+        else:
+            cp(v("W2", 0, 256), ind(Sg, v("eu")))
+            act(v("val"), ind(Sv, v("LU", 48, 64)), Fn.Identity)
         mm(v("B6", 0, 256), v("F"), v("em"), False, True)
         if not last:
-            tops_a(t + 1)
-        tt(v("nc"), v("B6", 0, 256), v("W2", 0, 256), Op.min)
-        cp(ind(Sw, v("LU", 0, 16)), v("nc"))
+            mm(v("B0", 0, 256), v("DT"), v("val"), True, True)
+        act(v("nc"), v("B6", 0, 256), Fn.Relu, -512.0)
         if not last:
-            tops_b(t + 1)
+            ts(prod(t + 1), v("B0", 0, 256), 0.0, Op.max)
+        tt(ind(Sw, v("LU", 16, 32)), v("W2", 0, 256), v("nc"), Op.add)
+        if last:
+            fill(6)
+        else:
+            tops(t + 1)
 
     n = 0
     home = lambda r, h: ext(T.y[32 * r:32 * r + 32, 1280 * h:1280 * h + 1280])
@@ -436,26 +456,24 @@ def rank_program(g, core, T, topo):
         for h in range(2):
             bk = v("B%d" % (n % 8), 0, 320)
             for j in range(4):
-                c = 1280 * h + 320 * j
-                mm(bk, v("SO", 128 * r + 3 - j, 128 * r + 131 - j), v("S", c, c + 320), j == 0, j == 3)
+                c = SB + (1280 * h + 320 * j if r in far else 640 * j + 320 * h)
+                mm(bk, v("SO", 128 * r + 3 - j, 128 * r + 131 - j), v("S", c, c + 320), False, j == 3)
             z = v("zt", 320 * n, 320 * n + 320)
             act(z, bk, Fn.Relu, 65536.0, -256.0)
             tt(tile("yo", r, h), bk, z, Op.min)
             n += 1
-        if r in far:
-            fused([(hp[(r, h)], e_all[8 * h:8 * h + 8], tile("yo", r, h), T.hY[:], "hY") for h in range(2)])
-        elif r == near:
+            if r in far:
+                fused([(hp[(r, h)], e_all, tile("yo", r, h), T.hY[:], "hY")])
+        if r == near:
             fused([(nc_, e_off, v("yo", 640 * r, 640 * r + 640), T.aN[:], "gY%d" % (2 * me))])
-        else:
-            for h in range(2):
-                dma("S", home(me, h), tile("yo", me, h), "st")
+        elif r == me:
+            dma("S", ext(rows(T.y, me)), v("yo", 640 * r, 640 * r + 640), "st")
     for r in far[::-1]:
         for h in range(2):
             arrive([slot("aY", 2 * r + h)], "gY%d" % (2 * r + h), n_off)
             dma("Y", home(r, h), slot("aY", 2 * r + h), "st")
     arrive([v("aN")], "gY%d" % (2 * near), n_off)
-    for h in range(2):
-        dma("S", home(near, h), v("aN", 320 * h, 320 * h + 320), "st")
+    dma("S", ext(rows(T.y, near)), v("aN"), "st")
     _emit(g, T, ops, queue)
 
 

from concourse.bass import DstId, RemoteDMATransfer
from concourse.mybir import AluOpType as Op, AxisListType, ActivationFunctionType as Fn

V, W, SB, DUM, WIN, BIG = 2560, 2048, 256, 2560, 5376, 4096.0
STEP = (1, 2, 3, 1)
MS, MX = 10, 12
LA, LB = 9, 4
CS = 96


def _sb(n, d):
    return ("sbuf", [128, n], {"b": "bfloat16", "f": "float32", "i": "int32", "u": "uint16"}[d])


SCRATCH = {}
for _d, _l in (("b", dict(S=WIN, pin=2560, yo=2560, zt=2560, I=128, nI=128, tm=128, tn=128, Big=576, BigW=144, BR=512, NP=512, RB=512,
                          DT=128, F=128, SI=896, SO=528, kk=256, c256=320, thr=256, nl=16, ask=16, bl=16, idle=16, cst=80,
                          BI=128, BRw=128 * (16 - MS), dS=2048, cmp=4096, brep=512, EQ=4096, ES=1024, W2=512, val=256, em=256,
                          prod=512, crem=256, rl=256, nc=256)),
               ("f", dict(If=128, vt=16, Xf=64, TRf=64, xi=2064, xs=528, xg=128, xm=256, cf=16, cd=32, wl=16, rst=256,
                          wrep=256, msel=256, t1=256, t2=256, base=80, lm=16, LF=80, b97=16, K=256,
                          R=256, ef=16, Df=256, ab=1024, sc=256)),
               ("i", dict(P=1024, TR=64, p4=4, ci=16, X=256, XA=256, ki=32)),
               ("u", dict(ex=16, ex15=4, LU=80, O=256, eu=16, D=256))):
    for _n, _w in _l.items():
        SCRATCH[_n] = _sb(_w, _d)
for _n, _k, _w in (("T", 8, 8), ("A", 4, 64), ("B", 4, 192)):
    SCRATCH.update({"d" + _n: ("dram", [_k, 128, _w], "int32"), "a" + _n: ("dram", [_k, 128, _w], "int32"), "h" + _n: ("dram", [128, _w], "int32")})
SCRATCH.update({
    "dD": ("dram", [8, 128, 320], "bfloat16"), "aY": ("dram", [8, 128, 320], "bfloat16"), "aN": ("dram", [128, 640], "bfloat16"),
    "hD": ("dram", [128, 320], "bfloat16"), "hY": ("dram", [128, 320], "bfloat16"),
})
for _b in range(8):
    SCRATCH["B%d" % _b] = ("psum", [128, 512], "float32")

SEMAPHORES = (["cV", "cS", "cT", "cG", "lA", "lC", "lX", "lB", "lS", "lM", "lN", "lT", "s2", "st", "sent", "gA", "gB", "gT", "hT",
               "hA", "hB", "hD", "hY"] + ["gD%d" % i for i in range(8)] + ["gY%d" % i for i in range(8)])


def _bits(engs):
    m = 0
    for e in engs:
        m |= 1 << e
    return m


def _helpers(T, topo, core):
    out = {}
    far = [q for q, c in enumerate(T.cores) if c != core and not topo.may_write(core, c)]
    for n, q in enumerate(far):
        own = [c for c in topo.cores_of(core) if T.rank_of(c) is None and topo.may_write(c, T.cores[q])]
        dies = sorted(set(topo.die(c) for c in own))
        for h in range(2):
            same = [c for c in own if topo.die(c) == dies[h % len(dies)]]
            out[(q, h)] = same[n % len(same)]
    return out


def _helper_program(g, core, T, topo):
    home = [c for c in topo.cores_of(core) if T.rank_of(c) is not None]
    if not home:
        return
    r = T.rank_of(home[0])
    jobs = [k for k, c in _helpers(T, topo, home[0]).items() if c == core]
    if not jobs:
        return
    q, h = jobs[0]
    dst = T.cores[q]
    rid, pid = topo.addr(dst, core)
    m = topo.mask(core, dst)
    n = len(topo.engines(core, dst))
    k = 2 * r + h
    x = "AB"[h]
    steps = [("hT", 1, T.hT[:], T.aT[k], "gT"), ("hD", 2, T.hD[:], T.pin[:, 320 * k:320 * k + 320], "gD%d" % k),
             ("h" + x, 4, T["h" + x][:], T["a" + x][r], "g" + x), ("hY", len(topo.engines(home[0], core)), T.hY[:], T.aY[k], "gY%d" % k)]
    for s, cnt, src, out, rs in steps:
        g.wait_ge(T.sem[s], cnt)
        g.remote_dma(out, src, T.sem[rs], T.sem.sent, pid, rid, m)
    g.wait_ge(T.sem.sent, n * len(steps))


def rank_program(g, core, T, topo):
    me = T.rank_of(core)
    if me is None:
        _helper_program(g, core, T, topo)
        return
    ops = []
    queue = {"V": g.vector, "S": g.scalar, "T": g.tensor, "G": g, "Y": g.sync}

    def v(name, a=None, b=None, s=1, p=None):
        t = T[name]
        if a is None:
            a, b = 0, t.shape[1]
        ps = slice(None) if p is None else slice(p[0], p[1])
        x = t[ps, a:b] if s == 1 else t[ps, a:b:s]
        p0, p1 = p if p else (0, 128)
        return (x, [(name, a, b, p0, p1, s == 1)])

    def slot(name, i, n=1):
        return (T[name][i] if n == 1 else T[name][i:i + n], [(name + "_", i, i + n, 0, 128, True)])

    def ind(win, off):
        return (win[0].indirect(off[0]), win[1] + off[1], win[1], off[1])

    def ap(x):
        return x[0] if isinstance(x, tuple) else x

    def rec(q, fn, outs, ins, sem=None, cnt=0, inc=True):
        wr, rd = [], []
        for o in outs:
            if len(o) == 4:
                wr += [x[:5] + (False,) for x in o[2]]
                rd += o[3]
            else:
                wr += o[1]
        for x in ins:
            if isinstance(x, tuple):
                rd += x[1]
        ops.append({"q": q, "fn": fn, "wr": wr, "rd": rd, "sem": sem, "cnt": cnt, "inc": inc})

    def tt(o, a, b, op): rec("V", lambda: g.vector.tensor_tensor(o[0], a[0], b[0], op), [o], [a, b])

    def ts(o, a, s1, op0, s2=None, op1=None):
        if s2 is None:
            rec("V", lambda: g.vector.tensor_scalar(o[0], a[0], ap(s1), None, op0), [o], [a, s1])
        else:
            rec("V", lambda: g.vector.tensor_scalar(o[0], a[0], ap(s1), ap(s2), op0, op1), [o], [a, s1, s2])

    def cp(o, a): rec("V", lambda: g.vector.tensor_copy(o[0], a[0]), [o], [a])
    def ms(o, c): rec("V", lambda: g.vector.memset(o[0], c), [o], [])
    def scan(o, a, b, init, op0, op1): rec("V", lambda: g.vector.tensor_tensor_scan(o[0], a[0], b[0], init, op0, op1), [o], [a, b])
    def act(o, a, f, bias=0.0, scale=1.0): rec("S", lambda: g.scalar.activation(o[0], a[0], f, ap(bias), ap(scale)), [o], [a, bias, scale])
    def mm(o, l, r, st, en): rec("T", lambda: g.tensor.matmul(o[0], l[0], r[0], st, en), [o], [l, r])

    def iota(o, pat, base, cm, flag=True):
        if flag:
            rec("G", lambda: g.iota(o[0], pat, base, cm, allow_small_or_imprecise_dtypes=True), [o], [])
        else:
            rec("G", lambda: g.iota(o[0], pat, base, cm), [o], [])

    def dma(q, o, a, sem): rec(q, lambda: queue[q].dma_start(o[0], a[0]), [o], [a], sem, 16)
    def arrive(o, sem, cnt): rec(None, None, o, [], sem, cnt)
    def ext(x): return (x, [])

    def fused(items, ls="sent", outs=()):
        trs = []
        for c, engs, src, out, rs in items:
            rid, pid = topo.addr(c, core)
            trs.append(RemoteDMATransfer(dst_ids=[DstId(rid=rid, pnc=pid)], dma_engine_mask=_bits(engs), remote_sem=T.sem[rs], src=src[0], dst=out))
        rec("G", lambda: g.remote_dma_fused(trs, local_sem=T.sem[ls]), list(outs), [it[2] for it in items], ls, sum(len(it[1]) for it in items), False)

    hp = _helpers(T, topo, core)
    far = sorted(set(q for q, h in hp), key=lambda q: (q - me) % len(T.cores))
    near = [q for q in range(len(T.cores)) if q != me and q not in far][0]
    nc_ = T.cores[near]
    e_off = topo.engines(core, nc_)
    e_all = topo.engines(core, hp[(far[0], 0)])
    e_on = [e for e in e_all if e not in e_off]
    n_off = len(e_off)
    hk = [(q, h) for q in far for h in range(2)]
    others = far + [near]
    mine = (32 * me, 32 * me + 32)
    days = lambda q, h: T.days[32 * q:32 * q + 32, 1280 * h:1280 * h + 1280]
    rows = lambda x, q: x[32 * q:32 * q + 32, :]
    tile = lambda name, r, h: v(name, 640 * r + 320 * h, 640 * r + 320 * h + 320)

    def numbers(x, h):
        fused([(hp[(q, h)], e_on[4 * n:4 * n + 4], slot("d" + x, q), T["h" + x][:], "h" + x) for n, q in enumerate(far)]
              + [(nc_, e_off, slot("d" + x, near), T["a" + x][me], "g" + x)])
    dma("S", slot("dT", 0, 8), ext(T.trucks[:, :]), "lC")
    for q in others:
        for h in range(2):
            dma("Y", slot("dD", 2 * q + h), ext(days(q, h)), "lX")
    dma("Y", slot("dA", 0, 4), ext(T.cand[:, 0:256]), "lA")
    dma("Y", v("pin", 640 * me, 640 * me + 640), ext(rows(T.days, me)), "lS")
    sent_far = (None, [("gate", 0, 1, 0, 128, True)])

    iota(v("p4"), [[32, 4]], 0, 1, False)
    iota(v("xs", 0, 256), [[1, 256]], 0, 0)
    iota(v("xg"), [[16, 8], [0, 16]], 0, 0)
    fused([(hp[k], e_on[n:n + 1], slot("dT", 2 * k[0] + k[1]), T.hT[:], "hT") for n, k in enumerate(hk)]
          + [(nc_, e_off[2 * h:2 * h + 1], slot("dT", 2 * near + h), T.aT[2 * me + h], "gT") for h in range(2)])
    fused([(hp[k], e_on[n::4], slot("dD", 2 * k[0] + k[1]), T.hD[:], "hD") for n, k in enumerate(hk)]
          + [(nc_, e_off[4 * h:4 * h + 4], slot("dD", 2 * near + h), tile("pin", me, h)[0], "gD%d" % (2 * me)) for h in range(2)], "s2", [sent_far])
    numbers("A", 0)
    dma("Y", v("TR", 0, 64, p=mine), (rows(T.trucks, me), sent_far[1]), "lT")
    dma("Y", v("P", 0, 1024, p=mine), ext(rows(T.cand, me)), "lM")
    for q in others:
        dma("Y", slot("dB", q), ext(T.cand[32 * q:32 * q + 32, 256:1024]), "lB")
    iota(v("xi"), [[1, 2064]], 0, 0)
    numbers("B", 1)
    iota(v("S", SB + DUM, WIN), [[0, WIN - SB - DUM]], 0, 0)

    arrive([slot("aT", 2 * r, 2) for r in others], "gT", 2 + 4 * n_off)
    for x in "AB":
        arrive([slot("a" + x, r) for r in others], "g" + x, 3 * n_off)
    arrive([tile("pin", near, 0), tile("pin", near, 1)], "gD%d" % (2 * near), n_off)
    for r in far:
        for h in range(2):
            arrive([tile("pin", r, h)], "gD%d" % (2 * r + h), n_off)
    for r in others:
        dma("Y", v("TR", 0, 64, p=(32 * r, 32 * r + 32)), slot("aT", 2 * r, 2), "lT")
    for r in others:
        dma("Y", v("P", 0, 256, p=(32 * r, 32 * r + 32)), slot("aA", r), "lM")
    for r in others:
        dma("Y", v("P", 256, 1024, p=(32 * r, 32 * r + 32)), slot("aB", r), "lN")

    col = lambda name, j: v(name, j, j + 1)
    ts(v("ci", 0, 4), v("p4"), 127, Op.bitwise_and)
    ts(v("ci", 4, 8), v("p4"), 112, Op.bitwise_and)
    ts(col("ci", 8), col("p4", 0), 15, Op.bitwise_and)
    ts(col("ci", 9), col("p4", 0), 3, Op.bitwise_and)
    ts(col("ci", 10), col("p4", 0), 2, Op.logical_shift_right)
    cp(v("cf", 0, 11), v("ci", 0, 11))
    pf, rf = col("cf", 0), col("cf", 8)
    ts(col("cd", 4), col("cf", 10), 96.0, Op.add)
    ts(v("cd", 12, 16), v("xs", 0, 4), col("cf", 9), Op.is_equal, -1.0, Op.mult)
    for j in range(4):
        ts(v("SI", 224 * j, 224 * j + 224), v("xs", 0, 224), col("cd", 4), Op.is_equal, col("cd", 12 + j), Op.mult)
    ts(v("cd", 0, 4), v("cf", 4, 8), 15.0, Op.add)
    ts(col("cd", 5), pf, 4.0, Op.mult, 3.0, Op.add)
    ts(col("cd", 11), rf, 15.0, Op.is_equal, 256.0, Op.mult)
    ts(col("cd", 7), pf, -1.0, Op.add)
    ts(col("cd", 8), pf, 1.0, Op.add)
    ts(col("cd", 9), rf, 0.0, Op.not_equal, -256.0, Op.mult)
    ts(col("cd", 10), rf, 15.0, Op.not_equal, 512.0, Op.mult)
    ts(col("cd", 16), rf, 0.0, Op.is_equal)
    ts(col("cd", 18), rf, 16.0, Op.mult, 15.0, Op.add)
    ts(col("cd", 6), col("cd", 11), 3840.0, Op.mult, 65536.0, Op.add)
    act(col("cd", 24), rf, Fn.Sigmoid, 580.0, -40.0)
    ts(v("I"), v("xs", 0, 128), pf, Op.is_equal)
    ms(v("c256"), 256.0)
    ts(v("If"), v("xs", 0, 128), pf, Op.is_equal)
    ts(v("nI"), v("xs", 0, 128), pf, Op.is_equal, -1.0, Op.mult)
    ts(v("tm"), v("xs", 0, 128), pf, Op.is_equal, 512.0, Op.mult)
    ts(v("tn"), v("xs", 0, 128), col("cd", 7), Op.is_equal, col("cd", 9), Op.mult)
    ts(v("F"), v("xs", 0, 128), col("cd", 8), Op.is_equal, col("cd", 10), Op.mult)
    for e in range(4):
        ts(v("Big", 144 * e, 144 * e + 144), v("xs", 0, 144), col("cd", e), Op.is_equal)
        ts(v("BR", 128 * e, 128 * e + 128), v("xg"), col("cf", 4 + e), Op.is_equal)
    tt(v("DT"), v("I"), v("tn"), Op.add)
    tt(v("F"), v("tm"), v("F"), Op.subtract)
    for e in range(1, 4):
        ts(v("NP", 128 * e, 128 * e + 128), v("xs", 0, 128), col("cf", e), Op.is_equal)
        ts(v("RB", 128 * e, 128 * e + 128), v("xs", 0, 128), col("cf", 4 - e), Op.is_equal, float(DUM), Op.mult)
    ts(v("BigW"), v("xs", 0, 144), col("cd", 0), Op.is_equal, col("cd", 6), Op.mult)
    ts(v("S", 0, SB), v("xs", 0, 256), col("cd", 16), Op.mult)
    ts(v("ex"), v("xs", 0, 16), 0.0, Op.mult, rf, Op.add)
    ts(v("ex15"), v("xs", 0, 4), 0.0, Op.mult, col("cd", 18), Op.add)
    ts(v("lm"), v("xs", 0, 16), 16.0, Op.mult, rf, Op.add)
    ms(v("t1"), 1.0 / 1.8)
    ms(v("t2"), 0.0)
    ts(v("base", 16, 32), v("lm"), float(DUM), Op.add)
    ts(v("base", 64, 80), v("lm"), 256.0, Op.add)
    ms(v("cst", 0, 16), -float(DUM))
    ms(v("cst", 16, 64), 0.0)
    cp(v("cst", 64, 80), v("lm"))
    ts(v("BI"), v("I"), BIG, Op.mult)
    scan(v("wrep"), v("t1"), v("t2"), 1.8e29, Op.mult, Op.add)
    for a, b in ((256, 512), (512, 528)):
        act(v("xs", a, b), v("xs", 0, b - a), Fn.Identity, float(a))
    for a in (0, 128):
        tt(v("xm", a, a + 128), v("xs", 0, 128), v("xg"), Op.subtract)
        act(v("kk", a, a + 128), v("xg"), Fn.Identity, 128.0 * a, 128.0)
    ts(v("SO"), v("xs"), col("cd", 5), Op.is_equal, -1.0, Op.mult)
    ts(v("msel"), v("xm"), rf, Op.is_equal)
    ts(v("rst"), v("xm"), 0.0, Op.not_equal, -9e29, Op.mult)
    tt(v("t1"), v("wrep"), v("msel"), Op.mult)
    rec("V", lambda: g.vector.tensor_reduce(T.cd[:, 19:20], T.t1[:, 0:16], AxisListType.X, Op.add), [col("cd", 19)], [v("t1", 0, 16)])
    ts(v("thr"), v("t1"), -2.5, Op.mult)
    ts(col("cd", 20), col("cd", 19), 1e-29, Op.mult)
    ts(v("wl"), v("wrep", 0, 256, 16), col("cd", 20), Op.mult)
    for m in range(MS, 16):
        ts(v("BRw", 128 * (m - MS), 128 * (m - MS) + 128), v("BR", 0, 128), col("wl", m), Op.mult)

    def fill(b): mm(v("B%d" % b, 0, 320), v("I"), v("c256"), True, False)

    def sel_in(r, b, en):
        j, x = (b % 4, b // 4) if r != me else (b // 2, b % 2)
        mm(v("B%d" % b, 0, 320), v("SI", 224 * j + 96 - 32 * r, 224 * j + 224 - 32 * r), tile("pin", r, x), False, en)
    for b in range(8):
        fill(b)
    for r in (me, near):
        for b in range(8):
            sel_in(r, b, False)
    for b in range(8):
        sel_in(far[0], b, False)
        sel_in(far[1], b, True)
        z = v("zt", 320 * b, 320 * b + 320)
        act(z, v("B%d" % b, 0, 320), Fn.Relu, 65536.0, -256.0)
        if b == 7:
            ts(v("LU", 48, 64), v("TR", 0, 16), float(SB), Op.add)
        tt(v("S", SB + 320 * b, SB + 320 * b + 320), v("B%d" % b, 0, 320), z, Op.min)

    I, nI = v("I"), v("nI")
    Sv, Sg, Sw = v("S", 0, SB + V), v("S", SB, SB + V), v("S", SB, WIN)
    prod = lambda t: v("prod", 256 * (t % 2), 256 * (t % 2) + 256)

    def listify(out, big, c0, src, a, b, first=True, end=True):
        for r in range(16):
            mm(out, v(big, c0 + 15 - r, c0 + 143 - r), v(src, a + r, b, 16), first and r == 0, end and r == 15)

    def tops(t):
        e = STEP[t]
        a = 256 * (t % 2)
        br = v("BR", 128 * e, 128 * e + 128)
        listify(v("B1", 0, 16), "Big", 144 * e, "prod", a, a + 256)
        mm(v("B2", 0, 256), br, prod(t), True, True)
        mm(v("B2", 256, 512), br, prod(t), True, True)
        mm(v("B7", 0, 256), I, v("val"), True, False)
        mm(v("B7", 0, 256), nI, prod(t), False, True)
        act(v("b97"), v("B1", 0, 16), Fn.Identity, 97.0 * 256, -97.0)
        act(v("brep"), v("B2"), Fn.Identity, 0.0, col("cd", 24))
        if t < 3:
            act(v("bl"), v("B1", 0, 16), Fn.Identity)
        act(v("crem") if t == 0 else v("W2", 256, 512), v("B7", 0, 256), Fn.Identity)

    act(v("val"), ind(Sv, v("LU", 48, 64)), Fn.Identity)
    cp(v("TRf"), v("TR"))
    mm(v("B0", 0, 256), v("DT"), v("val"), True, True)
    ts(prod(0), v("B0", 0, 256), 0.0, Op.max)
    tops(0)
    for t in range(4):
        e, last = STEP[t], t == 3
        n = 32 if last else 80
        src = v("TRf", 0, 16) if t == 0 else v("LF", 32, 48)
        def xo(a, b): tt(v("X", a, b), ind(v("b97"), v("ex", 0, (b - a) // 16)), v("P", 256 * t + a, 256 * t + b), Op.add)
        def xa(a, b): ts(v("XA", a, b), v("X", a, b), W - 1, Op.bitwise_and)
        def xu(a, b): cp(v("O", a, b), v("XA", a, b))
        rep = lambda a, b: v("brep", 16 * a % 256, 16 * a % 256 + 16 * (b - a))
        def gv(a, b): tt(v("cmp", 16 * a, 16 * b), ind(Sg, v("O", a, b)), rep(a, b), Op.is_gt)
        def gs(a, b): act(v("dS", 16 * a, 16 * b), ind(Sg, v("O", a, b)), Fn.Identity)
        def df(a, b, bk):
            o = v(bk, 0, 16 * (b - a))
            mm(o, nI, rep(a, b), True, False)
            mm(o, I, v("dS", 16 * a, 16 * b), False, True)
        def sg(a, b, bk): act(v("cmp", 16 * a, 16 * b), v(bk, 0, 16 * (b - a)), Fn.Sigmoid, -20.0, 40.0)
        def lead(a, bk):
            mm(v(bk, 0, 64), I, v("kk", a, a + 64), True, False)
            if a == 64:
                mm(v(bk, 0, 64), v("If"), v("Xf"), False, False)
        def score(a, bk): listify(v(bk, 0, 64), "BigW", 0, "cmp", 16 * a, 16 * a + 1024, False, True)
        def key(a, bk): tt(v("K", a, a + 64), v(bk, 0, 64), v("X", a, a + 64), Op.add)

        xo(0, 64); xo(192, 256); xa(0, 64); xa(192, 256); xu(0, 64); xu(192, 256); xo(64, 192)
        gs(0, 32)
        df(0, 32, "B3")
        gs(32, 64)
        for a, bk in ((192, "B5"), (0, "B6"), (128, "B2")):
            lead(a, bk)
        df(32, 64, "B4")
        sg(0, 32, "B3")
        sg(32, 64, "B4")
        gv(224, 256); xa(64, 192); gv(192, 224); xu(64, 192)
        cp(v("Xf"), v("X", 64, 128))
        gv(160, 192)
        score(192, "B5")
        gs(64, CS)
        lead(64, "B1")
        mm(v("B0", 0, 256), nI, v("brep", 0, 256), True, False)
        score(0, "B6")
        df(64, CS, "B3")
        if t > 0:
            act(v("crem"), ind(v("W2"), v("LU", 64, 80)), Fn.Identity)
        gv(128, 160)
        key(192, "B5")
        score(128, "B2"); sg(64, CS, "B3")
        gv(CS, 128)
        rb = v("RB", 128 * e, 128 * e + 128)
        lst = lambda i: v("B4" if i else "B5", 16 * i, 16 * i + 16)
        mm(v("B0", 0, 256), v("NP", 128 * e, 128 * e + 128), v("crem"), False, True)
        score(64, "B1")
        act(v("rl"), v("B0", 0, 256), Fn.Relu)
        listify(v("B7", 0, 16), "Big", 0, "rl", 0, 256)
        act(v("idle"), v("B7", 0, 16), Fn.Relu, BIG, -BIG)
        mm(v("B3", 0, 256), I, v("thr"), True, False)
        key(0, "B6")
        key(128, "B2")
        tt(v("R", 0, 64), v("K", 0, 64), v("K", 192, 256), Op.min)
        tt(v("R", 64, 96), v("K", 128, 160), v("K", 160, 192), Op.min)
        tt(v("R", 96, 128), v("R", 0, 32), v("R", 32, 64), Op.min)
        tt(v("R", 128, 160), v("R", 64, 96), v("R", 96, 128), Op.min)
        tt(v("R", 160, 192), v("B1", 0, 32), v("R", 128, 160), Op.min)
        tt(v("R", 192, 224), v("B1", 32, 64), v("R", 160, 192), Op.min)
        tt(v("ki", 0, 16), v("R", 192, 208), v("R", 208, 224), Op.min)
        ts(v("ki", 16, 32), v("ki", 0, 16), 0x1007FF, Op.bitwise_and)
        ts(v("eu"), v("ki", 16, 32), float(W), Op.min)
        tt(v("ef"), v("ki", 16, 32), v("idle"), Op.add)
        cp(v("D", 128, 256), ind(v("xi"), v("eu", 8, 16)))
        cp(v("D", 0, 128), ind(v("xi"), v("eu", 0, 8)))
        mm(lst(0), I, v("cst", 0, 16), True, False)
        mm(v("B4", 16, n), I, v("cst", 16, n), True, False)
        mm(lst(0), v("If"), src, False, False)
        if not last:
            mm(lst(3), I, v("bl"), False, False)
        mm(v("B6", 0, 256), v("BR", 128 * e, 128 * e + 128), prod(t), True, False)
        m0 = MS - MS % 2
        act(v("Df", 0, 256 - 16 * m0), ind(v("xi"), v("eu", m0, 16)), Fn.Identity)
        eq = lambda m: v("EQ", 272 * m, 256 * m + 256)
        pos = lambda m: sum(256 - 16 * x for x in range(MS, m))
        for a, b in ((MS, MX), (MX, 16)):
            for m in range(a, b):
                act(v("ab", pos(m), pos(m + 1)), v("Df", 16 * (m - m0), 256 - 16 * m0), Fn.Abs, col("ef", m), -1.0)
            act(v("ES", pos(a), pos(b)), v("ab", pos(a), pos(b)), Fn.Relu, 1.0, -1.0)
        act(v("ask"), v("B7", 0, 16), Fn.Sign)
        if not last:
            act(v("base", 32, 48), v("TRf", 16 * t + 16, 16 * t + 32), Fn.Identity)
            act(v("base", 48, 64), v("TRf", 16 * t + 16, 16 * t + 32), Fn.Identity, float(SB))

        def late(a, b):
            for m in range(a, b):
                mm(v("B3", 16 * m, 256), v("BRw", 128 * (m - MS), 128 * (m - MS) + 128), v("ES", pos(m), pos(m + 1)), False, False)
        for m in list(range(8, MS)) + list(range(8)):
            ts(eq(m), v("D", 16 * m, 256), col("ef", m), Op.is_equal, col("wl", m), Op.mult)
            mm(v("B3", 16 * m, 256), v("BR", 0, 128), eq(m), False, m == 7)
            if m == LA:
                late(MS, MX)
            if m == LB:
                late(MX, 16)
        mm(lst(0), rb, v("ask"), False, False)
        for i in range(1, 2 if last else 3):
            mm(lst(i), v("If"), v("ef"), False, False)
        ts(v("vt"), v("ef"), float(W), Op.is_ge, -4e29, Op.mult)
        scan(v("sc"), v("rst"), v("B3", 0, 256), 0.0, Op.max, Op.min)
        tt(v("nl"), ind(v("sc"), v("ex15", 0, 1)), v("vt"), Op.is_ge)
        mm(lst(0), rb, v("nl"), False, True)
        for i in range(1, n // 16):
            mm(lst(i), v("BI"), v("nl"), False, i == n // 16 - 1)
        cp(v("LU", 0, 16), lst(0))
        tt(v("LF", 16, n), v("B4", 16, n), v("base", 16, n), Op.min)
        cp(ind(Sw, v("LU", 0, 16)), v("crem"))
        cp(v("LU", 16, n), v("LF", 16, n))
        ts(v("em"), ind(Sg, v("eu")), 0.5, Op.is_lt)
        if last:
            act(v("W2", 0, 256), ind(Sg, v("eu")), Fn.Identity)
            for b in (0, 1, 2, 3, 4, 5, 7):
                fill(b)
        else:
            cp(v("W2", 0, 256), ind(Sg, v("eu")))
            act(v("val"), ind(Sv, v("LU", 48, 64)), Fn.Identity)
        mm(v("B6", 0, 256), v("F"), v("em"), False, True)
        if not last:
            mm(v("B0", 0, 256), v("DT"), v("val"), True, True)
        act(v("nc"), v("B6", 0, 256), Fn.Relu, -512.0)
        if not last:
            ts(prod(t + 1), v("B0", 0, 256), 0.0, Op.max)
        tt(ind(Sw, v("LU", 16, 32)), v("W2", 0, 256), v("nc"), Op.add)
        if last:
            fill(6)
        else:
            tops(t + 1)

    n = 0
    home = lambda r, h: ext(T.y[32 * r:32 * r + 32, 1280 * h:1280 * h + 1280])
    for r in far + [near, me]:
        for h in range(2):
            bk = v("B%d" % (n % 8), 0, 320)
            for j in range(4):
                c = SB + (1280 * h + 320 * j if r in far else 640 * j + 320 * h)
                mm(bk, v("SO", 128 * r + 3 - j, 128 * r + 131 - j), v("S", c, c + 320), False, j == 3)
            z = v("zt", 320 * n, 320 * n + 320)
            act(z, bk, Fn.Relu, 65536.0, -256.0)
            tt(tile("yo", r, h), bk, z, Op.min)
            n += 1
            if r in far:
                fused([(hp[(r, h)], e_all, tile("yo", r, h), T.hY[:], "hY")])
        if r == near:
            fused([(nc_, e_off, v("yo", 640 * r, 640 * r + 640), T.aN[:], "gY%d" % (2 * me))])
        elif r == me:
            dma("S", ext(rows(T.y, me)), v("yo", 640 * r, 640 * r + 640), "st")
    for r in far[::-1]:
        for h in range(2):
            arrive([slot("aY", 2 * r + h)], "gY%d" % (2 * r + h), n_off)
            dma("Y", home(r, h), slot("aY", 2 * r + h), "st")
    arrive([v("aN")], "gY%d" % (2 * near), n_off)
    dma("S", ext(rows(T.y, near)), v("aN"), "st")
    _emit(g, T, ops, queue)


def _emit(g, T, ops, queue):
    total, log = {}, {}
    for o in ops:
        if o["sem"]:
            total[o["sem"]] = total.get(o["sem"], 0) + o["cnt"]
    known = {q: {} for q in queue}
    for i, o in enumerate(ops):
        q = o["q"]
        need = []
        for regs, wr in ((o["rd"], False), (o["wr"], True)):
            for nm, a, b, p0, p1, full in regs:
                ps = nm[0] == "B" and nm[1:].isdigit()
                for j, a2, b2, r0, r1, w2 in log.get(nm, []):
                    if j == i:
                        continue
                    if ps:
                        hit = ops[j]["q"] != q
                    else:
                        hit = (wr or w2) and a < b2 and a2 < b and p0 < r1 and r0 < p1
                    if hit:
                        need.append(j)
        for regs, wr in ((o["rd"], False), (o["wr"], True)):
            for nm, a, b, p0, p1, full in regs:
                ps = nm[0] == "B" and nm[1:].isdigit()
                old = log.get(nm, [])
                if ps:
                    old = [x for x in old if ops[x[0]]["q"] == q and q != "T"]
                elif wr and full:
                    old = [x for x in old if not (a <= x[1] and x[2] <= b and p0 <= x[3] and x[4] <= p1)]
                log[nm] = old + [(i, a, b, p0, p1, wr)]
        o["waits"] = []
        if q is not None:
            kn = known[q]
            top = {}
            for j in need:
                d = ops[j]
                if d["sem"]:
                    top[d["sem"]] = j
                else:
                    if d["q"] != "T":
                        d["mark"] = True
                    top["c" + d["q"]] = max(top.get("c" + d["q"], -1), j)
            for s, j in sorted(top.items(), key=lambda x: -x[1]):
                lvl = 10 ** 9 if ops[j]["sem"] else j
                if kn.get(s, -1) >= lvl:
                    continue
                ops[j]["mark"] = True
                o["waits"].append((s, j))
                kn[s] = lvl
                if not ops[j]["sem"]:
                    for s2, l2 in ops[j]["clock"].items():
                        kn[s2] = max(kn.get(s2, -1), l2)
            o["clock"] = dict(kn)
    cnt = {}
    for o in ops:
        if not o["sem"] and o.get("mark"):
            s = "c" + o["q"]
            cnt[s] = cnt.get(s, 0) + 1
            o["n"] = cnt[s]
    for o in ops:
        if o["q"] is None:
            continue
        for s, j in o["waits"]:
            queue[o["q"]].wait_ge(T.sem[s], total[s] if ops[j]["sem"] else ops[j]["n"])
        ins = o["fn"]()
        if o["sem"]:
            if o["inc"]:
                ins.then_inc(T.sem[o["sem"]], 16)
        elif o.get("mark"):
            ins.then_inc(T.sem["c" + o["q"]], 1)
    for s, n in list(cnt.items()) + list(total.items()):
        g.wait_ge(T.sem[s], n)
